import numpy as np
import ml_dtypes


def mxq(x, axis, fmt="e4m3"):
    dtype, down = {"e4m3": (ml_dtypes.float8_e4m3fn, 7), "e5m2": (ml_dtypes.float8_e5m2, 14)}[fmt]
    v = np.moveaxis(np.asarray(x, np.float32).astype(ml_dtypes.bfloat16).astype(np.float64), axis, -1)
    blocks = v.reshape(v.shape[:-1] + (-1, 32))
    amax = np.abs(blocks).max(-1, keepdims=True)
    byte = np.maximum(np.where(amax > 0, np.frexp(amax)[1] - 1 + 127, 0) - down, 1)
    scale = np.exp2(byte - 127.0)
    codes = (blocks / scale).astype(np.float32).astype(dtype).astype(np.float64)
    return np.moveaxis((codes * scale).reshape(v.shape), -1, axis)


WIDE = False


def mx_kscale(k):
    if not WIDE:
        return np.ones(k)
    levels = np.array([10, -10, 5, -5, 0])
    if k % 512:
        return np.exp2(np.random.permutation(np.resize(levels, k // 32))).repeat(32)
    a = np.empty((k // 512, 16))
    for p in range(k // 512):
        a[p, :8] = np.random.permutation(np.resize(levels, 8))
        for g in range(8):
            far = levels[np.abs(levels - a[p, g]) >= 10]
            a[p, g + 8] = far[np.random.randint(len(far))]
    return np.exp2(a.ravel()).repeat(32)


def f64(x):
    return np.asarray(x).astype(np.float64)


def striped(idx):
    return np.tile(idx.reshape(-1, 16).T, (8, 1)).astype(np.uint16)


def unstriped(offs):
    return offs[:16].T.reshape(-1).astype(np.int64)


def pack_weight(w):
    k, n = w.shape
    w = f64(np.asarray(w, np.float32).astype(ml_dtypes.bfloat16)).reshape(k // 32, 32, n)
    amax = np.abs(w).max(1)
    byte = np.clip(np.where(amax > 0, np.frexp(amax)[1] - 1 + 127 - 7, 1), 1, 254)
    scaled = (w * np.exp2(127.0 - byte)[:, None, :]).reshape(k, n).astype(np.float32)
    words = np.ascontiguousarray(scaled.reshape(k // 512, 128, 4, n).transpose(0, 1, 3, 2)).astype(ml_dtypes.float8_e4m3fn).view(np.uint8)
    return words, np.ascontiguousarray(byte.astype(np.uint8).reshape(k // 512, 16, n))


def unpack_weight(words, scales):
    g, p, n, _ = words.shape
    vals = np.ascontiguousarray(words).view(ml_dtypes.float8_e4m3fn).astype(np.float64) * np.repeat(np.exp2(scales.astype(np.float64) - 127.0), 8, axis=1)[..., None]
    return vals.transpose(0, 1, 3, 2).reshape(g * 512, n)


def gelu(v):
    return 0.5 * v * (1.0 + np.tanh(np.sqrt(2.0 / np.pi) * (v + 0.044715 * v**3)))

def planes(y):
    n, m = y.shape
    v = y.astype(np.float32).astype(ml_dtypes.bfloat16).astype(np.float64).reshape(n // 32, 32, m)
    top = np.abs(v).max(1)
    byte = np.clip(np.where(top > 0, np.frexp(top)[1] - 1 + 127 - 7, 1), 1, 254)
    codes = (v * np.exp2(127.0 - byte)[:, None, :]).reshape(n, m).astype(np.float32).astype(ml_dtypes.float8_e4m3fn).view(np.uint8)
    words = codes.reshape(n // 512, 128, 4, m).transpose(0, 1, 3, 2)
    return np.ascontiguousarray(words), np.ascontiguousarray(byte.astype(np.uint8).reshape(n // 512, 16, m))


K, T, N, U = 512, 512, 512, 1024
P = 2 ** 7


def setup_inputs():
    n = np.random.standard_normal
    s = mx_kscale(K)[:, None]
    packed_xT = pack_weight(n((K, T)) * s)
    return {
        "x_words": packed_xT[0],
        "x_scales": packed_xT[1],
        "gate": np.tile(np.random.uniform(0.5, 1.5, T), (P, 1)).astype(np.float32),
        "w1": (n((K, N)) / np.sqrt(K) / s).astype(np.float32),
        "dst": striped(np.random.permutation(U)[:T]),
    }


def reference(x_words, x_scales, gate, w1, dst):
    xq = unpack_weight(x_words, x_scales)
    y = gelu(mxq(f64(w1), 0, "e4m3").T @ xq)
    out = np.zeros((N, U))
    out[:, unstriped(dst)] = y * f64(gate)[:1]
    return (out,) + planes(out)

@@ -1,0 +1,150 @@
+from contextlib import ExitStack
+
+import concourse.mybir as mybir
+
+K, T, N, U = 512, 512, 512, 1024
+FLOPS = 2 * K * T * N
+
+F32 = mybir.dt.float32
+BF16 = mybir.dt.bfloat16
+I32 = mybir.dt.int32
+U32 = mybir.dt.uint32
+U16 = mybir.dt.uint16
+U8 = mybir.dt.uint8
+FP8X4 = mybir.dt.float8_e4m3fn_x4
+GELU = mybir.ActivationFunctionType.Gelu_apprx_tanh
+MULT = mybir.AluOpType.mult
+
+P = 128
+PACK = 4
+QUADRANTS = 4
+LIST_ROWS = 16
+CHUNK = 256
+CHUNKS = U // CHUNK
+
+
+def tile_picked_wroute2_lingelu_lo_kernel(
+    tc, x_words, x_scales, gate, w1, dst, out_0, out_1, out_2
+):
+    nc = tc.nc
+    with ExitStack() as ctx:
+        pool = ctx.enter_context(tc.tile_pool(name="pool", bufs=1))
+        psum = ctx.enter_context(tc.psum_pool(name="psum", bufs=1))
+
+        offsets = pool.tile([P, T // LIST_ROWS], U16, name="offsets")
+        x_codes = pool.tile([P, T], U32, name="x_codes", align_bytes=64)
+        x_plane = pool.tile([P, T], U8, name="x_plane", align_bytes=64)
+        gate_sb = pool.tile([P, T], F32, name="gate_sb")
+        w_raw = [pool.tile([P, 2, N], F32, name=f"w_raw{h}") for h in range(2)]
+        windows = [pool.tile([P, U], F32, name=f"window{t}") for t in range(PACK)]
+
+        w_rows = w1.rearrange("(p j) n -> p j n", j=PACK)
+        for h in range(2):
+            nc.sync.dma_start(w_raw[h][:], w_rows[:, 2 * h : 2 * h + 2, :])
+        nc.sync.dma_start(x_codes[:].bitcast(I32), x_words[0].rearrange("p n r -> p (n r)").bitcast(I32))
+        nc.sync.dma_start(offsets[:], dst)
+        nc.sync.dma_start(gate_sb[:], gate)
+
+        nc.vector.memset(x_plane[:].bitcast(U32), 0)
+        for q in range(QUADRANTS):
+            nc.scalar.dma_start(
+                x_plane[32 * q : 32 * q + 4, :].bitcast(I32),
+                x_scales[0, 4 * q : 4 * q + 4, :].bitcast(I32),
+            )
+
+        warm_in = pool.tile([P, 1], F32, name="warm_in")
+        warm_out = pool.tile([P, 1], F32, name="warm_out")
+        nc.vector.memset(warm_in[:], 0.0)
+        nc.scalar.activation(warm_out[:], warm_in[:], GELU)
+
+        for t in range(PACK):
+            nc.vector.memset(windows[t][:], 0.0)
+
+        groups = ((0, 1), (1, 2), (2, 4))
+        w_bf = [pool.tile([P, b - a, P, PACK], BF16, name=f"w_bf{a}", align_bytes=64) for a, b in groups]
+        w_codes = [pool.tile([P, (b - a) * P], U32, name=f"w_codes{a}", align_bytes=64) for a, b in groups]
+        w_plane = [pool.tile([P, (b - a) * P], U8, name=f"w_plane{a}", align_bytes=64) for a, b in groups]
+
+        def round_weights(g, h):
+            a, b = groups[g]
+            src = w_raw[h][:].rearrange("p j (m t) -> p m j t", t=PACK)[:, :, :, a:b]
+            dst_view = w_bf[g][:].rearrange("p t m j -> p m j t")[:, :, 2 * h : 2 * h + 2, :]
+            if g == 2:
+                nc.scalar.copy(dst_view, src)
+            else:
+                nc.vector.tensor_copy(dst_view, src)
+
+        def quantize_weights(g):
+            nc.vector.quantize_mx(
+                out=w_codes[g][:].bitcast(FP8X4),
+                scales=w_plane[g][:],
+                in_=w_bf[g][:].rearrange("p t m j -> p (t m j)"),
+            )
+
+        for g in range(3):
+            round_weights(g, 0)
+        round_weights(2, 1)
+        for g in range(2):
+            round_weights(g, 1)
+            quantize_weights(g)
+        quantize_weights(2)
+
+        pieces = [(t, 0, T) for t in range(PACK)]
+        ys = []
+        for t, c0, c1 in pieces:
+            g = min(t, 2)
+            m0 = (t - groups[g][0]) * P
+            acc = psum.tile([P, c1 - c0], F32, name=f"acc{t}_{c0}")
+            nc.tensor.matmul_mx(
+                out=acc[:],
+                lhsT=w_codes[g][:, m0 : m0 + P].bitcast(FP8X4),
+                lhsT_scale=w_plane[g][:, m0 : m0 + P],
+                rhs=x_codes[:, c0:c1].bitcast(FP8X4),
+                rhs_scale=x_plane[:, c0:c1],
+                start=True,
+                stop=True,
+            )
+            y = pool.tile([P, c1 - c0], F32, name=f"y{t}_{c0}")
+            nc.scalar.activation(y[:], acc[:], GELU)
+            ys.append(y)
+
+        grouped = [pool.tile([P, CHUNK, PACK], BF16, name=f"grouped{c}", align_bytes=64) for c in range(CHUNKS)]
+        out_rows = out_0.rearrange("(p t) u -> p t u", t=PACK)
+        for (t, c0, c1), y in zip(pieces, ys):
+            nc.vector.tensor_tensor(
+                windows[t][:].indirect(offsets[:, c0 // LIST_ROWS : c1 // LIST_ROWS]),
+                y[:],
+                gate_sb[:, c0:c1],
+                MULT,
+            )
+            if c1 < T:
+                continue
+            nc.sync.dma_start(out_rows[:, t, :], windows[t][:])
+            for c in range(CHUNKS):
+                src = windows[t][:, c * CHUNK : (c + 1) * CHUNK]
+                if t == PACK - 1 and c < CHUNKS // 2:
+                    nc.vector.tensor_copy(grouped[c][:, :, t], src)
+                elif t == PACK - 2 and c < CHUNKS // 2:
+                    both = src.rearrange("p (u o) -> p u o", o=1).to_broadcast([P, CHUNK, 2])
+                    nc.scalar.copy(grouped[c][:, :, t:], both)
+                else:
+                    nc.scalar.copy(grouped[c][:, :, t], src)
+
+        stores = ((0, 2), (2, 3), (3, 4))
+        o_codes = [pool.tile([P, (b - a) * CHUNK], U32, name=f"o_codes{a}", align_bytes=64) for a, b in stores]
+        o_plane = pool.tile([P, U], U8, name="o_plane", align_bytes=64)
+        words_out = out_1[0].rearrange("p u r -> p (u r)").bitcast(I32)
+        for (a, b), codes in zip(stores, o_codes):
+            for c in range(a, b):
+                nc.vector.quantize_mx(
+                    out=codes[:, (c - a) * CHUNK : (c - a + 1) * CHUNK].bitcast(FP8X4),
+                    scales=o_plane[:, c * CHUNK : (c + 1) * CHUNK],
+                    in_=grouped[c][:].rearrange("p u t -> p (u t)"),
+                )
+            nc.sync.dma_start(words_out[:, a * CHUNK : b * CHUNK], codes[:].bitcast(I32))
+        for q in range(QUADRANTS):
+            queue = nc.scalar if q < 2 else nc.sync
+            queue.dma_start(
+                out_2[0, 4 * q : 4 * q + 4, :].bitcast(I32),
+                o_plane[32 * q : 32 * q + 4, :].bitcast(I32),
+            )

@@ -35,8 +35,8 @@ def tile_picked_wroute2_lingelu_lo_kernel(
         x_codes = pool.tile([P, T], U32, name="x_codes", align_bytes=64)
         x_plane = pool.tile([P, T], U8, name="x_plane", align_bytes=64)
         gate_sb = pool.tile([P, T], F32, name="gate_sb")
-        w_raw = [pool.tile([P, 2, N], F32, name=f"w_raw{h}") for h in range(2)]
-        windows = [pool.tile([P, U], F32, name=f"window{t}") for t in range(PACK)]
+        w_raw = [pool.tile([P, 2, N], F32, name=f"w_raw{h}", tag=f"w_raw{h}", align_bytes=64) for h in range(2)]
+        windows = [pool.tile([P, U], F32, name=f"window{t}") for t in range(3)]
 
         w_rows = w1.rearrange("(p j) n -> p j n", j=PACK)
         for h in range(2):
@@ -45,7 +45,6 @@ def tile_picked_wroute2_lingelu_lo_kernel(
         nc.sync.dma_start(offsets[:], dst)
         nc.sync.dma_start(gate_sb[:], gate)
 
-        nc.vector.memset(x_plane[:].bitcast(U32), 0)
         for q in range(QUADRANTS):
             nc.scalar.dma_start(
                 x_plane[32 * q : 32 * q + 4, :].bitcast(I32),
@@ -57,11 +56,11 @@ def tile_picked_wroute2_lingelu_lo_kernel(
         nc.vector.memset(warm_in[:], 0.0)
         nc.scalar.activation(warm_out[:], warm_in[:], GELU)
 
-        for t in range(PACK):
+        for t in range(3):
             nc.vector.memset(windows[t][:], 0.0)
 
         groups = ((0, 1), (1, 2), (2, 4))
-        w_bf = [pool.tile([P, b - a, P, PACK], BF16, name=f"w_bf{a}", align_bytes=64) for a, b in groups]
+        w_bf = [pool.tile([P, b - a, P, PACK], BF16, name=f"w_bf{a}", tag=f"w_bf{a}", align_bytes=64) for a, b in groups]
         w_codes = [pool.tile([P, (b - a) * P], U32, name=f"w_codes{a}", align_bytes=64) for a, b in groups]
         w_plane = [pool.tile([P, (b - a) * P], U8, name=f"w_plane{a}", align_bytes=64) for a, b in groups]
 
@@ -88,24 +87,30 @@ def tile_picked_wroute2_lingelu_lo_kernel(
             round_weights(g, 1)
             quantize_weights(g)
         quantize_weights(2)
+        for t, tag in ((3, "w_raw1"),):
+            windows.append(pool.tile([P, U], F32, name=f"window{t}", tag=tag, align_bytes=64))
+            nc.vector.memset(windows[t][:], 0.0)
 
         pieces = [(t, 0, T) for t in range(PACK)]
         ys = []
-        for t, c0, c1 in pieces:
+        for t in range(PACK):
             g = min(t, 2)
             m0 = (t - groups[g][0]) * P
-            acc = psum.tile([P, c1 - c0], F32, name=f"acc{t}_{c0}")
-            nc.tensor.matmul_mx(
-                out=acc[:],
-                lhsT=w_codes[g][:, m0 : m0 + P].bitcast(FP8X4),
-                lhsT_scale=w_plane[g][:, m0 : m0 + P],
-                rhs=x_codes[:, c0:c1].bitcast(FP8X4),
-                rhs_scale=x_plane[:, c0:c1],
-                start=True,
-                stop=True,
-            )
-            y = pool.tile([P, c1 - c0], F32, name=f"y{t}_{c0}")
-            nc.scalar.activation(y[:], acc[:], GELU)
+            y = pool.tile([P, T], F32, name=f"y{t}")
+            width = T // 2 if t == 0 else T
+            for c0 in range(0, T, width):
+                cols = slice(c0, c0 + width)
+                acc = psum.tile([P, width], F32, name=f"acc{t}_{c0}")
+                nc.tensor.matmul_mx(
+                    out=acc[:],
+                    lhsT=w_codes[g][:, m0 : m0 + P].bitcast(FP8X4),
+                    lhsT_scale=w_plane[g][:, m0 : m0 + P],
+                    rhs=x_codes[:, cols].bitcast(FP8X4),
+                    rhs_scale=x_plane[:, cols],
+                    start=True,
+                    stop=True,
+                )
+                nc.scalar.activation(y[:, cols], acc[:], GELU)
             ys.append(y)
 
         grouped = [pool.tile([P, CHUNK, PACK], BF16, name=f"grouped{c}", align_bytes=64) for c in range(CHUNKS)]

@@ -19,8 +19,9 @@ P = 128
 PACK = 4
 QUADRANTS = 4
 LIST_ROWS = 16
-CHUNK = 256
-CHUNKS = U // CHUNK
+SHARED = 8
+CHUNKS = ((0, 512), (512, 768), (768, 1024))
+VECTOR_PLACES = 576
 
 
 def tile_picked_wroute2_lingelu_lo_kernel(
@@ -35,8 +36,8 @@ def tile_picked_wroute2_lingelu_lo_kernel(
         x_codes = pool.tile([P, T], U32, name="x_codes", align_bytes=64)
         x_plane = pool.tile([P, T], U8, name="x_plane", align_bytes=64)
         gate_sb = pool.tile([P, T], F32, name="gate_sb")
-        w_raw = [pool.tile([P, 2, N], F32, name=f"w_raw{h}", tag=f"w_raw{h}", align_bytes=64) for h in range(2)]
-        windows = [pool.tile([P, U], F32, name=f"window{t}") for t in range(3)]
+        w_raw = [pool.tile([P, 2, N], F32, name=f"w_raw{h}", align_bytes=64) for h in range(2)]
+        windows = [pool.tile([P, U], F32, name=f"window{t}") for t in range(2)]
 
         w_rows = w1.rearrange("(p j) n -> p j n", j=PACK)
         for h in range(2):
@@ -44,67 +45,62 @@ def tile_picked_wroute2_lingelu_lo_kernel(
         nc.sync.dma_start(x_codes[:].bitcast(I32), x_words[0].rearrange("p n r -> p (n r)").bitcast(I32))
         nc.sync.dma_start(offsets[:], dst)
         nc.sync.dma_start(gate_sb[:], gate)
-
         for q in range(QUADRANTS):
             nc.scalar.dma_start(
                 x_plane[32 * q : 32 * q + 4, :].bitcast(I32),
                 x_scales[0, 4 * q : 4 * q + 4, :].bitcast(I32),
             )
 
-        warm_in = pool.tile([P, 1], F32, name="warm_in")
-        warm_out = pool.tile([P, 1], F32, name="warm_out")
-        nc.vector.memset(warm_in[:], 0.0)
-        nc.scalar.activation(warm_out[:], warm_in[:], GELU)
-
-        for t in range(3):
+        for t in range(2):
             nc.vector.memset(windows[t][:], 0.0)
 
+        w_bf = pool.tile([P, PACK * P - SHARED, PACK], BF16, name="w_bf", tag="w_bf", align_bytes=64)
+        first = w_bf[:, 0:P, :].rearrange("p (t m) j -> p t m j", t=1)
+        rest = w_bf[:, P - SHARED :, :].rearrange("p (t m) j -> p t m j", t=PACK - 1)
         groups = ((0, 1), (1, 2), (2, 4))
-        w_bf = [pool.tile([P, b - a, P, PACK], BF16, name=f"w_bf{a}", tag=f"w_bf{a}", align_bytes=64) for a, b in groups]
-        w_codes = [pool.tile([P, (b - a) * P], U32, name=f"w_codes{a}", align_bytes=64) for a, b in groups]
-        w_plane = [pool.tile([P, (b - a) * P], U8, name=f"w_plane{a}", align_bytes=64) for a, b in groups]
+        w_codes = pool.tile([P, PACK * P], U32, name="w_codes", align_bytes=64)
+        w_planes = [pool.tile([P, (b - a) * P], U8, name=f"w_plane{a}", align_bytes=64) for a, b in groups]
 
-        def round_weights(g, h):
-            a, b = groups[g]
-            src = w_raw[h][:].rearrange("p j (m t) -> p m j t", t=PACK)[:, :, :, a:b]
-            dst_view = w_bf[g][:].rearrange("p t m j -> p m j t")[:, :, 2 * h : 2 * h + 2, :]
-            if g == 2:
-                nc.scalar.copy(dst_view, src)
-            else:
-                nc.vector.tensor_copy(dst_view, src)
+        def rounded(a, b):
+            return first if a == 0 else rest[:, a - 1 : b - 1]
+
+        def round_weights(h, a, b, m0=0, m1=P):
+            src = w_raw[h][:].rearrange("p j (m t) -> p m t j", t=PACK)[:, m0:m1, a:b, :]
+            nc.vector.tensor_copy(rounded(a, b).rearrange("p t m j -> p m t j")[:, m0:m1, :, 2 * h : 2 * h + 2], src)
 
         def quantize_weights(g):
+            a, b = groups[g]
             nc.vector.quantize_mx(
-                out=w_codes[g][:].bitcast(FP8X4),
-                scales=w_plane[g][:],
-                in_=w_bf[g][:].rearrange("p t m j -> p (t m j)"),
+                out=w_codes[:, a * P : b * P].bitcast(FP8X4),
+                scales=w_planes[g][:],
+                in_=rounded(a, b).rearrange("p t m j -> p (t m j)"),
             )
 
-        for g in range(3):
-            round_weights(g, 0)
-        round_weights(2, 1)
-        for g in range(2):
-            round_weights(g, 1)
-            quantize_weights(g)
+        round_weights(0, 0, 1)
+        round_weights(0, 1, 2, SHARED, P)
+        round_weights(0, 2, PACK)
+        round_weights(1, 0, 1)
+        quantize_weights(0)
+        round_weights(1, 1, PACK)
+        round_weights(0, 1, 2, 0, SHARED)
+        quantize_weights(1)
         quantize_weights(2)
-        for t, tag in ((3, "w_raw1"),):
-            windows.append(pool.tile([P, U], F32, name=f"window{t}", tag=tag, align_bytes=64))
-            nc.vector.memset(windows[t][:], 0.0)
+        windows.append(pool.tile([P, U], F32, name="window2", tag="w_bf", align_bytes=64))
+        nc.gpsimd.memset(windows[2][:], 0.0)
 
-        pieces = [(t, 0, T) for t in range(PACK)]
         ys = []
         for t in range(PACK):
             g = min(t, 2)
             m0 = (t - groups[g][0]) * P
-            y = pool.tile([P, T], F32, name=f"y{t}")
-            width = T // 2 if t == 0 else T
+            y = pool.tile([P, T], F32, name=f"y{t}", tag=f"y{t}")
+            width = P if t == 0 else T
             for c0 in range(0, T, width):
                 cols = slice(c0, c0 + width)
                 acc = psum.tile([P, width], F32, name=f"acc{t}_{c0}")
                 nc.tensor.matmul_mx(
                     out=acc[:],
-                    lhsT=w_codes[g][:, m0 : m0 + P].bitcast(FP8X4),
-                    lhsT_scale=w_plane[g][:, m0 : m0 + P],
+                    lhsT=w_codes[:, t * P : (t + 1) * P].bitcast(FP8X4),
+                    lhsT_scale=w_planes[g][:, m0 : m0 + P],
                     rhs=x_codes[:, cols].bitcast(FP8X4),
                     rhs_scale=x_plane[:, cols],
                     start=True,
@@ -113,40 +109,37 @@ def tile_picked_wroute2_lingelu_lo_kernel(
                 nc.scalar.activation(y[:, cols], acc[:], GELU)
             ys.append(y)
 
-        grouped = [pool.tile([P, CHUNK, PACK], BF16, name=f"grouped{c}", align_bytes=64) for c in range(CHUNKS)]
+        grouped = [pool.tile([P, b - a, PACK], BF16, name=f"grouped{a}", align_bytes=64) for a, b in CHUNKS]
         out_rows = out_0.rearrange("(p t) u -> p t u", t=PACK)
-        for (t, c0, c1), y in zip(pieces, ys):
-            nc.vector.tensor_tensor(
-                windows[t][:].indirect(offsets[:, c0 // LIST_ROWS : c1 // LIST_ROWS]),
-                y[:],
-                gate_sb[:, c0:c1],
-                MULT,
-            )
-            if c1 < T:
-                continue
+        for t in range(PACK):
+            if t == PACK - 1:
+                windows.append(pool.tile([P, U], F32, name="window3", tag="y0"))
+                nc.gpsimd.memset(windows[3][:], 0.0)
+            nc.vector.tensor_tensor(windows[t][:].indirect(offsets[:]), ys[t][:], gate_sb[:], MULT)
             nc.sync.dma_start(out_rows[:, t, :], windows[t][:])
-            for c in range(CHUNKS):
-                src = windows[t][:, c * CHUNK : (c + 1) * CHUNK]
-                if t == PACK - 1 and c < CHUNKS // 2:
-                    nc.vector.tensor_copy(grouped[c][:, :, t], src)
-                elif t == PACK - 2 and c < CHUNKS // 2:
-                    both = src.rearrange("p (u o) -> p u o", o=1).to_broadcast([P, CHUNK, 2])
-                    nc.scalar.copy(grouped[c][:, :, t:], both)
-                else:
-                    nc.scalar.copy(grouped[c][:, :, t], src)
+            for (a, b), tile in zip(CHUNKS, grouped):
+                cuts = (a, VECTOR_PLACES, b) if t >= PACK - 2 and a < VECTOR_PLACES < b else (a, b)
+                for u0, u1 in zip(cuts, cuts[1:]):
+                    src = windows[t][:, u0:u1]
+                    target = tile[:, u0 - a : u1 - a, :]
+                    if t == PACK - 1 and u1 <= VECTOR_PLACES:
+                        nc.vector.tensor_copy(target[:, :, t], src)
+                    elif t == PACK - 2 and u1 <= VECTOR_PLACES:
+                        both = src.rearrange("p (u o) -> p u o", o=1).to_broadcast([P, u1 - u0, 2])
+                        nc.scalar.copy(target[:, :, t:], both)
+                    else:
+                        nc.scalar.copy(target[:, :, t], src)
 
-        stores = ((0, 2), (2, 3), (3, 4))
-        o_codes = [pool.tile([P, (b - a) * CHUNK], U32, name=f"o_codes{a}", align_bytes=64) for a, b in stores]
         o_plane = pool.tile([P, U], U8, name="o_plane", align_bytes=64)
         words_out = out_1[0].rearrange("p u r -> p (u r)").bitcast(I32)
-        for (a, b), codes in zip(stores, o_codes):
-            for c in range(a, b):
-                nc.vector.quantize_mx(
-                    out=codes[:, (c - a) * CHUNK : (c - a + 1) * CHUNK].bitcast(FP8X4),
-                    scales=o_plane[:, c * CHUNK : (c + 1) * CHUNK],
-                    in_=grouped[c][:].rearrange("p u t -> p (u t)"),
-                )
-            nc.sync.dma_start(words_out[:, a * CHUNK : b * CHUNK], codes[:].bitcast(I32))
+        for (a, b), tile in zip(CHUNKS, grouped):
+            codes = pool.tile([P, b - a], U32, name=f"o_codes{a}", align_bytes=64)
+            nc.vector.quantize_mx(
+                out=codes[:].bitcast(FP8X4),
+                scales=o_plane[:, a:b],
+                in_=tile[:].rearrange("p u t -> p (u t)"),
+            )
+            nc.sync.dma_start(words_out[:, a:b], codes[:].bitcast(I32))
         for q in range(QUADRANTS):
             queue = nc.scalar if q < 2 else nc.sync
             queue.dma_start(

@@ -21,7 +21,7 @@ QUADRANTS = 4
 LIST_ROWS = 16
 SHARED = 8
 CHUNKS = ((0, 512), (512, 768), (768, 1024))
-VECTOR_PLACES = 576
+VECTOR_PLACES = 512
 
 
 def tile_picked_wroute2_lingelu_lo_kernel(
@@ -132,12 +132,13 @@ def tile_picked_wroute2_lingelu_lo_kernel(
 
         o_plane = pool.tile([P, U], U8, name="o_plane", align_bytes=64)
         words_out = out_1[0].rearrange("p u r -> p (u r)").bitcast(I32)
-        for (a, b), tile in zip(CHUNKS, grouped):
+        for c, a in ((1, 512), (0, 0), (0, 256), (2, 768)):
+            b = a + 256
             codes = pool.tile([P, b - a], U32, name=f"o_codes{a}", align_bytes=64)
             nc.vector.quantize_mx(
                 out=codes[:].bitcast(FP8X4),
                 scales=o_plane[:, a:b],
-                in_=tile[:].rearrange("p u t -> p (u t)"),
+                in_=grouped[c][:, a - CHUNKS[c][0] : b - CHUNKS[c][0], :].rearrange("p u t -> p (u t)"),
             )
             nc.sync.dma_start(words_out[:, a:b], codes[:].bitcast(I32))
         for q in range(QUADRANTS):

@@ -20,8 +20,9 @@ PACK = 4
 QUADRANTS = 4
 LIST_ROWS = 16
 SHARED = 8
-CHUNKS = ((0, 512), (512, 768), (768, 1024))
-VECTOR_PLACES = 512
+LATE = 88
+CHUNKS = ((0, 768), (768, 1024))
+VECTOR_PLACES = 576
 
 
 def tile_picked_wroute2_lingelu_lo_kernel(
@@ -80,9 +81,10 @@ def tile_picked_wroute2_lingelu_lo_kernel(
         round_weights(0, 1, 2, SHARED, P)
         round_weights(0, 2, PACK)
         round_weights(1, 0, 1)
+        round_weights(1, 1, PACK, LATE, P)
         quantize_weights(0)
-        round_weights(1, 1, PACK)
         round_weights(0, 1, 2, 0, SHARED)
+        round_weights(1, 1, PACK, 0, LATE)
         quantize_weights(1)
         quantize_weights(2)
         windows.append(pool.tile([P, U], F32, name="window2", tag="w_bf", align_bytes=64))
@@ -119,6 +121,8 @@ def tile_picked_wroute2_lingelu_lo_kernel(
             nc.sync.dma_start(out_rows[:, t, :], windows[t][:])
             for (a, b), tile in zip(CHUNKS, grouped):
                 cuts = (a, VECTOR_PLACES, b) if t >= PACK - 2 and a < VECTOR_PLACES < b else (a, b)
+                if t == PACK - 1 and a == 0:
+                    cuts = (a, 256) + cuts[1:]
                 for u0, u1 in zip(cuts, cuts[1:]):
                     src = windows[t][:, u0:u1]
                     target = tile[:, u0 - a : u1 - a, :]
@@ -132,7 +136,7 @@ def tile_picked_wroute2_lingelu_lo_kernel(
 
         o_plane = pool.tile([P, U], U8, name="o_plane", align_bytes=64)
         words_out = out_1[0].rearrange("p u r -> p (u r)").bitcast(I32)
-        for c, a in ((1, 512), (0, 0), (0, 256), (2, 768)):
+        for c, a in ((0, 0), (0, 256), (0, 512), (1, 768)):
             b = a + 256
             codes = pool.tile([P, b - a], U32, name=f"o_codes{a}", align_bytes=64)
             nc.vector.quantize_mx(

@@ -1,6 +1,7 @@
 from contextlib import ExitStack
 
 import concourse.mybir as mybir
+from concourse.masks import make_identity
 
 K, T, N, U = 512, 512, 512, 1024
 FLOPS = 2 * K * T * N
@@ -19,10 +20,11 @@ P = 128
 PACK = 4
 QUADRANTS = 4
 LIST_ROWS = 16
-SHARED = 8
-LATE = 88
+HALF = P // 2
+LEAD = 256
+TURN = 256
 CHUNKS = ((0, 768), (768, 1024))
-VECTOR_PLACES = 576
+VECTOR_PLACES = 704
 
 
 def tile_picked_wroute2_lingelu_lo_kernel(
@@ -37,90 +39,123 @@ def tile_picked_wroute2_lingelu_lo_kernel(
         x_codes = pool.tile([P, T], U32, name="x_codes", align_bytes=64)
         x_plane = pool.tile([P, T], U8, name="x_plane", align_bytes=64)
         gate_sb = pool.tile([P, T], F32, name="gate_sb")
-        w_raw = [pool.tile([P, 2, N], F32, name=f"w_raw{h}", align_bytes=64) for h in range(2)]
+        w_raw = [pool.tile([P, PACK, N // 2], F32, name=f"w_raw{h}", tag=f"w_raw{h}", align_bytes=64) for h in range(2)]
         windows = [pool.tile([P, U], F32, name=f"window{t}") for t in range(2)]
+        identity = pool.tile([P, P], F32, name="identity")
 
-        w_rows = w1.rearrange("(p j) n -> p j n", j=PACK)
-        for h in range(2):
-            nc.sync.dma_start(w_raw[h][:], w_rows[:, 2 * h : 2 * h + 2, :])
-        nc.sync.dma_start(x_codes[:].bitcast(I32), x_words[0].rearrange("p n r -> p (n r)").bitcast(I32))
-        nc.sync.dma_start(offsets[:], dst)
-        nc.sync.dma_start(gate_sb[:], gate)
         for q in range(QUADRANTS):
             nc.scalar.dma_start(
                 x_plane[32 * q : 32 * q + 4, :].bitcast(I32),
                 x_scales[0, 4 * q : 4 * q + 4, :].bitcast(I32),
             )
+        w_rows = w1.rearrange("(p j) n -> p j n", j=PACK)
+        x_rows = x_words[0].rearrange("p n r -> p (n r)").bitcast(I32)
+        nc.sync.dma_start(w_raw[0][:], w_rows[:, :, : N // 2])
+        nc.sync.dma_start(x_codes[:, :LEAD].bitcast(I32), x_rows[:, :LEAD])
+        nc.sync.dma_start(offsets[:], dst)
+        nc.sync.dma_start(gate_sb[:, :LEAD], gate[:, :LEAD])
+        nc.sync.dma_start(w_raw[1][:], w_rows[:, :, N // 2 :])
+        nc.sync.dma_start(x_codes[:, LEAD:].bitcast(I32), x_rows[:, LEAD:])
+        nc.sync.dma_start(gate_sb[:, LEAD:], gate[:, LEAD:])
 
+        make_identity(nc, identity[:])
         for t in range(2):
             nc.vector.memset(windows[t][:], 0.0)
 
-        w_bf = pool.tile([P, PACK * P - SHARED, PACK], BF16, name="w_bf", tag="w_bf", align_bytes=64)
-        first = w_bf[:, 0:P, :].rearrange("p (t m) j -> p t m j", t=1)
-        rest = w_bf[:, P - SHARED :, :].rearrange("p (t m) j -> p t m j", t=PACK - 1)
-        groups = ((0, 1), (1, 2), (2, 4))
-        w_codes = pool.tile([P, PACK * P], U32, name="w_codes", align_bytes=64)
-        w_planes = [pool.tile([P, (b - a) * P], U8, name=f"w_plane{a}", align_bytes=64) for a, b in groups]
+        w_codes = [pool.tile([P, P], U32, name=f"w_codes{s}", align_bytes=64) for s in range(PACK)]
+        w_planes = [pool.tile([P, P], U8, name=f"w_plane{s}", align_bytes=64) for s in range(PACK)]
 
-        def rounded(a, b):
-            return first if a == 0 else rest[:, a - 1 : b - 1]
+        def round_weights(h, copy):
+            low = pool.tile([P, P * PACK], BF16, name=f"w_low{h}", tag=f"w_low{h}", align_bytes=64)
+            high = pool.tile([P, P * PACK], BF16, name=f"w_high{h}", tag=f"w_high{h}", align_bytes=64)
+            src = w_raw[h][:].rearrange("p j (l t) -> p l j t", t=PACK)
+            copy(low[:].rearrange("p (l t j) -> p l j t", t=2, j=PACK), src[:, :, :, :2])
+            copy(high[:].rearrange("p (t l j) -> p l j t", t=2, j=PACK), src[:, :, :, 2:])
+            return low, high
 
-        def round_weights(h, a, b, m0=0, m1=P):
-            src = w_raw[h][:].rearrange("p j (m t) -> p m t j", t=PACK)[:, m0:m1, a:b, :]
-            nc.vector.tensor_copy(rounded(a, b).rearrange("p t m j -> p m t j")[:, m0:m1, :, 2 * h : 2 * h + 2], src)
-
-        def quantize_weights(g):
-            a, b = groups[g]
-            nc.vector.quantize_mx(
-                out=w_codes[:, a * P : b * P].bitcast(FP8X4),
-                scales=w_planes[g][:],
-                in_=rounded(a, b).rearrange("p t m j -> p (t m j)"),
-            )
-
-        round_weights(0, 0, 1)
-        round_weights(0, 1, 2, SHARED, P)
-        round_weights(0, 2, PACK)
-        round_weights(1, 0, 1)
-        round_weights(1, 1, PACK, LATE, P)
-        quantize_weights(0)
-        round_weights(0, 1, 2, 0, SHARED)
-        round_weights(1, 1, PACK, 0, LATE)
-        quantize_weights(1)
-        quantize_weights(2)
-        windows.append(pool.tile([P, U], F32, name="window2", tag="w_bf", align_bytes=64))
-        nc.gpsimd.memset(windows[2][:], 0.0)
-
-        ys = []
-        for t in range(PACK):
-            g = min(t, 2)
-            m0 = (t - groups[g][0]) * P
-            y = pool.tile([P, T], F32, name=f"y{t}", tag=f"y{t}")
-            width = P if t == 0 else T
-            for c0 in range(0, T, width):
-                cols = slice(c0, c0 + width)
-                acc = psum.tile([P, width], F32, name=f"acc{t}_{c0}")
-                nc.tensor.matmul_mx(
-                    out=acc[:],
-                    lhsT=w_codes[:, t * P : (t + 1) * P].bitcast(FP8X4),
-                    lhsT_scale=w_planes[g][:, m0 : m0 + P],
-                    rhs=x_codes[:, cols].bitcast(FP8X4),
-                    rhs_scale=x_plane[:, cols],
-                    start=True,
-                    stop=True,
+        def quantize_weights(h, low, high):
+            nc.vector.quantize_mx(out=w_codes[h][:].bitcast(FP8X4), scales=w_planes[h][:], in_=low[:])
+            cols = slice(h * HALF, (h + 1) * HALF)
+            for t in range(2):
+                nc.vector.quantize_mx(
+                    out=w_codes[2 + t][:, cols].bitcast(FP8X4),
+                    scales=w_planes[2 + t][:, cols],
+                    in_=high[:, t * HALF * PACK : (t + 1) * HALF * PACK],
                 )
-                nc.scalar.activation(y[:, cols], acc[:], GELU)
-            ys.append(y)
 
-        grouped = [pool.tile([P, b - a, PACK], BF16, name=f"grouped{a}", align_bytes=64) for a, b in CHUNKS]
-        out_rows = out_0.rearrange("(p t) u -> p t u", t=PACK)
-        for t in range(PACK):
-            if t == PACK - 1:
-                windows.append(pool.tile([P, U], F32, name="window3", tag="y0"))
-                nc.gpsimd.memset(windows[3][:], 0.0)
-            nc.vector.tensor_tensor(windows[t][:].indirect(offsets[:]), ys[t][:], gate_sb[:], MULT)
+        def project(s, y, c0, c1, bank):
+            acc = psum.tile([P, c1 - c0], F32, name=f"acc{s}_{c0}", tag=f"bank{bank}")
+            nc.tensor.matmul_mx(
+                out=acc[:],
+                lhsT=w_codes[s][:].bitcast(FP8X4),
+                lhsT_scale=w_planes[s][:],
+                rhs=x_codes[:, c0:c1].bitcast(FP8X4),
+                rhs_scale=x_plane[:, c0:c1],
+                start=True,
+                stop=True,
+            )
+            nc.scalar.activation(y, acc[:], GELU)
+
+        def scatter(s, y, c0, c1):
+            places = offsets[:, c0 // LIST_ROWS : c1 // LIST_ROWS]
+            nc.vector.tensor_tensor(windows[s][:].indirect(places), y, gate_sb[:, c0:c1], MULT)
+
+        quantize_weights(0, *round_weights(0, nc.vector.tensor_copy))
+        windows.append(pool.tile([P, U], F32, name="window2", tag="w_high0", align_bytes=64))
+        nc.gpsimd.memset(windows[2][:], 0.0)
+        y_lead = pool.tile([P, LEAD], F32, name="y_lead", tag="y_lead")
+        for c0 in range(0, LEAD, P):
+            project(0, y_lead[:, c0 : c0 + P], c0, c0 + P, c0 // P)
+        scatter(0, y_lead[:], 0, LEAD)
+
+        quantize_weights(1, *round_weights(1, nc.scalar.copy))
+        y_rest = pool.tile([P, T - LEAD], F32, name="y_rest", tag="w_raw1", align_bytes=64)
+        project(0, y_rest[:], LEAD, T, 2)
+        scatter(0, y_rest[:], LEAD, T)
+        ys = [pool.tile([P, T], F32, name=f"y{s}") for s in range(1, PACK)]
+        for c0 in range(0, T, T // 2):
+            project(1, ys[0][:, c0 : c0 + T // 2], c0, c0 + T // 2, 3 + c0 // (T // 2))
+        project(2, ys[1][:], 0, T, 5)
+        project(3, ys[2][:], 0, T, 6)
+        windows.append(pool.tile([P, U], F32, name="window3", tag="w_raw1", align_bytes=64))
+        nc.gpsimd.memset(windows[3][:], 0.0)
+
+        grouped = [pool.tile([P, (b - a) * PACK], BF16, name=f"grouped{a}", align_bytes=64) for a, b in CHUNKS]
+        turned = [pool.tile([P, TURN // P, 2, P], BF16, name=f"turned{k}") for k in range(U // TURN)]
+        out_rows = out_0.rearrange("(l t) u -> l t u", t=PACK)
+
+        def turn_out(h):
+            for k in range(U // TURN):
+                bank = psum.tile([P, TURN // P, P], F32, name=f"turn{h}_{k}", tag=f"bank{3 + k}")
+                for j in range(TURN // P):
+                    u0 = k * TURN + j * P
+                    nc.tensor.transpose(bank[:, j, :], windows[h][:, u0 : u0 + P], identity[:])
+                nc.scalar.copy(turned[k][:, :, h, :], bank[:])
+
+        def turn_back():
+            for k in range(U // TURN):
+                bank = psum.tile([P, TURN], F32, name=f"back{k}", tag=f"bank{(7 + k) % 8}")
+                words = turned[k][:].rearrange("p j h r -> p j (h r)").bitcast(F32)
+                for j in range(TURN // P):
+                    nc.tensor.transpose(bank[:, j * P : (j + 1) * P], words[:, j, :], identity[:])
+                c = 0 if k * TURN < CHUNKS[0][1] else 1
+                a = k * TURN - CHUNKS[c][0]
+                target = grouped[c][:].bitcast(F32).rearrange("p (u e) -> p u e", e=2)[:, a : a + TURN, :]
+                nc.scalar.copy(target, bank[:].rearrange("p (u o) -> p u o", o=1).to_broadcast([P, TURN, 2]))
+
+        nc.sync.dma_start(out_rows[:HALF, :2, :], windows[0][:])
+        turn_out(0)
+        scatter(1, ys[0][:], 0, T)
+        nc.sync.dma_start(out_rows[HALF:, :2, :], windows[1][:])
+        turn_out(1)
+        turn_back()
+
+        for t in range(2, PACK):
+            scatter(t, ys[t - 1][:], 0, T)
             nc.sync.dma_start(out_rows[:, t, :], windows[t][:])
-            for (a, b), tile in zip(CHUNKS, grouped):
-                cuts = (a, VECTOR_PLACES, b) if t >= PACK - 2 and a < VECTOR_PLACES < b else (a, b)
+            for (a, b), flat in zip(CHUNKS, grouped):
+                tile = flat[:].rearrange("p (u t) -> p u t", t=PACK)
+                cuts = (a, VECTOR_PLACES, b) if a < VECTOR_PLACES < b else (a, b)
                 if t == PACK - 1 and a == 0:
                     cuts = (a, 256) + cuts[1:]
                 for u0, u1 in zip(cuts, cuts[1:]):
@@ -142,7 +177,7 @@ def tile_picked_wroute2_lingelu_lo_kernel(
             nc.vector.quantize_mx(
                 out=codes[:].bitcast(FP8X4),
                 scales=o_plane[:, a:b],
-                in_=grouped[c][:, a - CHUNKS[c][0] : b - CHUNKS[c][0], :].rearrange("p u t -> p (u t)"),
+                in_=grouped[c][:, (a - CHUNKS[c][0]) * PACK : (b - CHUNKS[c][0]) * PACK],
             )
             nc.sync.dma_start(words_out[:, a:b], codes[:].bitcast(I32))
         for q in range(QUADRANTS):

@@ -14,7 +14,9 @@ U16 = mybir.dt.uint16
 U8 = mybir.dt.uint8
 FP8X4 = mybir.dt.float8_e4m3fn_x4
 GELU = mybir.ActivationFunctionType.Gelu_apprx_tanh
+COPY = mybir.ActivationFunctionType.Copy
 MULT = mybir.AluOpType.mult
+ADD = mybir.AluOpType.add
 
 P = 128
 PACK = 4
@@ -23,8 +25,8 @@ LIST_ROWS = 16
 HALF = P // 2
 LEAD = 256
 TURN = 256
-CHUNKS = ((0, 768), (768, 1024))
-VECTOR_PLACES = 704
+CHUNKS = ((0, 512), (512, 768), (768, 1024))
+VECTOR_PLACES = 512
 
 
 def tile_picked_wroute2_lingelu_lo_kernel(
@@ -70,7 +72,10 @@ def tile_picked_wroute2_lingelu_lo_kernel(
             high = pool.tile([P, P * PACK], BF16, name=f"w_high{h}", tag=f"w_high{h}", align_bytes=64)
             src = w_raw[h][:].rearrange("p j (l t) -> p l j t", t=PACK)
             copy(low[:].rearrange("p (l t j) -> p l j t", t=2, j=PACK), src[:, :, :, :2])
-            copy(high[:].rearrange("p (t l j) -> p l j t", t=2, j=PACK), src[:, :, :, 2:])
+            dealt = high[:].rearrange("p (t l j) -> p l j t", t=2, j=PACK)
+            step = HALF if h == 0 else HALF // 2
+            for l0 in range(0, HALF, step):
+                copy(dealt[:, l0 : l0 + step], src[:, l0 : l0 + step, :, 2:])
             return low, high
 
         def quantize_weights(h, low, high):
@@ -109,15 +114,41 @@ def tile_picked_wroute2_lingelu_lo_kernel(
         scatter(0, y_lead[:], 0, LEAD)
 
         quantize_weights(1, *round_weights(1, nc.scalar.copy))
-        y_rest = pool.tile([P, T - LEAD], F32, name="y_rest", tag="w_raw1", align_bytes=64)
+        y_rest = pool.tile([P, T - LEAD], F32, name="y_rest", tag="y_rest")
         project(0, y_rest[:], LEAD, T, 2)
         scatter(0, y_rest[:], LEAD, T)
         ys = [pool.tile([P, T], F32, name=f"y{s}") for s in range(1, PACK)]
         for c0 in range(0, T, T // 2):
             project(1, ys[0][:, c0 : c0 + T // 2], c0, c0 + T // 2, 3 + c0 // (T // 2))
         project(2, ys[1][:], 0, T, 5)
-        project(3, ys[2][:], 0, T, 6)
-        windows.append(pool.tile([P, U], F32, name="window3", tag="w_raw1", align_bytes=64))
+
+        gate_bank = psum.tile([P, T // P, P], F32, name="gate_bank", tag="bank7")
+        acc = psum.tile([P, T // P, P], F32, name="acc3", tag="bank6")
+        for c in range(T // P):
+            tokens = slice(c * P, (c + 1) * P)
+            nc.tensor.transpose(gate_bank[:, c, :], gate_sb[:, tokens], identity[:])
+        for c in range(T // P):
+            tokens = slice(c * P, (c + 1) * P)
+            nc.tensor.matmul_mx(
+                out=acc[:, c, :],
+                lhsT=x_codes[:, tokens].bitcast(FP8X4),
+                lhsT_scale=x_plane[:, tokens],
+                rhs=w_codes[3][:].bitcast(FP8X4),
+                rhs_scale=w_planes[3][:],
+                start=True,
+                stop=True,
+            )
+        gate_col = pool.tile([P, T // P], F32, name="gate_col")
+        nc.scalar.copy(gate_col[:], gate_bank[:, :, 0])
+        by_token = pool.tile([P, T // P, P], F32, name="by_token")
+        gated = pool.tile([P, T // P, P], F32, name="gated")
+        nc.scalar.activation(by_token[:], acc[:], GELU)
+        back = psum.tile([P, T // P, P], F32, name="back", tag="bank0")
+        for c in range(T // P):
+            nc.scalar.activation(gated[:, c, :], by_token[:, c, :], COPY, scale=gate_col[:, c : c + 1])
+            nc.tensor.transpose(back[:, c, :], gated[:, c, :], identity[:])
+        nc.scalar.copy(ys[2][:], back[:].rearrange("p c r -> p (c r)"))
+        windows.append(pool.tile([P, U], F32, name="window3", tag="y_rest"))
         nc.gpsimd.memset(windows[3][:], 0.0)
 
         grouped = [pool.tile([P, (b - a) * PACK], BF16, name=f"grouped{a}", align_bytes=64) for a, b in CHUNKS]
@@ -138,7 +169,7 @@ def tile_picked_wroute2_lingelu_lo_kernel(
                 words = turned[k][:].rearrange("p j h r -> p j (h r)").bitcast(F32)
                 for j in range(TURN // P):
                     nc.tensor.transpose(bank[:, j * P : (j + 1) * P], words[:, j, :], identity[:])
-                c = 0 if k * TURN < CHUNKS[0][1] else 1
+                c = max(c for c, (a, b) in enumerate(CHUNKS) if a <= k * TURN)
                 a = k * TURN - CHUNKS[c][0]
                 target = grouped[c][:].bitcast(F32).rearrange("p (u e) -> p u e", e=2)[:, a : a + TURN, :]
                 nc.scalar.copy(target, bank[:].rearrange("p (u o) -> p u o", o=1).to_broadcast([P, TURN, 2]))
@@ -150,28 +181,27 @@ def tile_picked_wroute2_lingelu_lo_kernel(
         turn_out(1)
         turn_back()
 
-        for t in range(2, PACK):
-            scatter(t, ys[t - 1][:], 0, T)
-            nc.sync.dma_start(out_rows[:, t, :], windows[t][:])
-            for (a, b), flat in zip(CHUNKS, grouped):
-                tile = flat[:].rearrange("p (u t) -> p u t", t=PACK)
-                cuts = (a, VECTOR_PLACES, b) if a < VECTOR_PLACES < b else (a, b)
-                if t == PACK - 1 and a == 0:
-                    cuts = (a, 256) + cuts[1:]
-                for u0, u1 in zip(cuts, cuts[1:]):
-                    src = windows[t][:, u0:u1]
-                    target = tile[:, u0 - a : u1 - a, :]
-                    if t == PACK - 1 and u1 <= VECTOR_PLACES:
-                        nc.vector.tensor_copy(target[:, :, t], src)
-                    elif t == PACK - 2 and u1 <= VECTOR_PLACES:
-                        both = src.rearrange("p (u o) -> p u o", o=1).to_broadcast([P, u1 - u0, 2])
-                        nc.scalar.copy(target[:, :, t:], both)
-                    else:
-                        nc.scalar.copy(target[:, :, t], src)
+        def places(u0, u1):
+            c = max(c for c, (a, b) in enumerate(CHUNKS) if a <= u0)
+            a = CHUNKS[c][0]
+            return grouped[c][:].rearrange("p (u t) -> p u t", t=PACK)[:, u0 - a : u1 - a, :]
+
+        scatter(2, ys[1][:], 0, T)
+        nc.sync.dma_start(out_rows[:, 2, :], windows[2][:])
+        both = windows[2][:, :VECTOR_PLACES].rearrange("p (u o) -> p u o", o=1).to_broadcast([P, VECTOR_PLACES, 2])
+        nc.gpsimd.tensor_scalar(places(0, VECTOR_PLACES)[:, :, 2:], both, 1.0, -0.0, MULT, ADD)
+        for a, b in CHUNKS[1:]:
+            nc.scalar.copy(places(a, b)[:, :, 2], windows[2][:, a:b])
+
+        nc.vector.tensor_copy(windows[3][:].indirect(offsets[:]), ys[2][:])
+        nc.sync.dma_start(out_rows[:, 3, :], windows[3][:])
+        for a in range(0, U, 256):
+            copy = nc.vector.tensor_copy if a < VECTOR_PLACES else nc.scalar.copy
+            copy(places(a, a + 256)[:, :, 3], windows[3][:, a : a + 256])
 
         o_plane = pool.tile([P, U], U8, name="o_plane", align_bytes=64)
         words_out = out_1[0].rearrange("p u r -> p (u r)").bitcast(I32)
-        for c, a in ((0, 0), (0, 256), (0, 512), (1, 768)):
+        for c, a in ((0, 0), (0, 256), (1, 512), (2, 768)):
             b = a + 256
             codes = pool.tile([P, b - a], U32, name=f"o_codes{a}", align_bytes=64)
             nc.vector.quantize_mx(

@@ -80,6 +80,9 @@ def tile_picked_wroute2_lingelu_lo_kernel(
 
         def quantize_weights(h, low, high):
             nc.vector.quantize_mx(out=w_codes[h][:].bitcast(FP8X4), scales=w_planes[h][:], in_=low[:])
+            quantize_high(h, high)
+
+        def quantize_high(h, high):
             cols = slice(h * HALF, (h + 1) * HALF)
             for t in range(2):
                 nc.vector.quantize_mx(
@@ -105,7 +108,20 @@ def tile_picked_wroute2_lingelu_lo_kernel(
             places = offsets[:, c0 // LIST_ROWS : c1 // LIST_ROWS]
             nc.vector.tensor_tensor(windows[s][:].indirect(places), y, gate_sb[:, c0:c1], MULT)
 
-        quantize_weights(0, *round_weights(0, nc.vector.tensor_copy))
+        first = w_raw[0][:].rearrange("p j (l t) -> p l j t", t=PACK)
+        lows = [
+            pool.tile([P, HALF * PACK], BF16, name=f"w_first{i}", tag=("w_high0", "w_low0")[i], align_bytes=64)
+            for i in range(2)
+        ]
+        for i, low in enumerate(lows):
+            words = slice(i * HALF // 2, (i + 1) * HALF // 2)
+            nc.vector.tensor_copy(low[:].rearrange("p (l t j) -> p l j t", t=2, j=PACK), first[:, words, :, :2])
+        for i, low in enumerate(lows):
+            cols = slice(i * HALF, (i + 1) * HALF)
+            nc.vector.quantize_mx(out=w_codes[0][:, cols].bitcast(FP8X4), scales=w_planes[0][:, cols], in_=low[:])
+        high = pool.tile([P, P * PACK], BF16, name="w_high0", tag="w_high0", align_bytes=64)
+        nc.vector.tensor_copy(high[:].rearrange("p (t l j) -> p l j t", t=2, j=PACK), first[:, :, :, 2:])
+        quantize_high(0, high)
         windows.append(pool.tile([P, U], F32, name="window2", tag="w_high0", align_bytes=64))
         nc.gpsimd.memset(windows[2][:], 0.0)
         y_lead = pool.tile([P, LEAD], F32, name="y_lead", tag="y_lead")

@@ -227,7 +227,7 @@ def tile_picked_wroute2_lingelu_lo_kernel(
             )
             nc.sync.dma_start(words_out[:, a:b], codes[:].bitcast(I32))
         for q in range(QUADRANTS):
-            queue = nc.scalar if q < 2 else nc.sync
+            queue = nc.scalar if q < 1 else nc.sync
             queue.dma_start(
                 out_2[0, 4 * q : 4 * q + 4, :].bitcast(I32),
                 o_plane[32 * q : 32 * q + 4, :].bitcast(I32),

@@ -1,7 +1,6 @@
 from contextlib import ExitStack
 
 import concourse.mybir as mybir
-from concourse.masks import make_identity
 
 K, T, N, U = 512, 512, 512, 1024
 FLOPS = 2 * K * T * N
@@ -23,10 +22,10 @@ PACK = 4
 QUADRANTS = 4
 LIST_ROWS = 16
 HALF = P // 2
-LEAD = 256
-TURN = 256
-CHUNKS = ((0, 512), (512, 768), (768, 1024))
-VECTOR_PLACES = 512
+LEAD = 128
+PIECE = T // 2
+CHUNK = 256
+CHUNKS = U // CHUNK
 
 
 def tile_picked_wroute2_lingelu_lo_kernel(
@@ -40,10 +39,9 @@ def tile_picked_wroute2_lingelu_lo_kernel(
         offsets = pool.tile([P, T // LIST_ROWS], U16, name="offsets")
         x_codes = pool.tile([P, T], U32, name="x_codes", align_bytes=64)
         x_plane = pool.tile([P, T], U8, name="x_plane", align_bytes=64)
-        gate_sb = pool.tile([P, T], F32, name="gate_sb")
-        w_raw = [pool.tile([P, PACK, N // 2], F32, name=f"w_raw{h}", tag=f"w_raw{h}", align_bytes=64) for h in range(2)]
-        windows = [pool.tile([P, U], F32, name=f"window{t}") for t in range(2)]
-        identity = pool.tile([P, P], F32, name="identity")
+        gate_sb = pool.tile([P, T], F32, name="gate_sb", tag="gate_sb")
+        w_raw = [pool.tile([P, PACK, N // 2], F32, name=f"w_raw{h}") for h in range(2)]
+        windows = [pool.tile([P, U], F32, name=f"window{t}") for t in range(PACK)]
 
         for q in range(QUADRANTS):
             nc.scalar.dma_start(
@@ -51,181 +49,114 @@ def tile_picked_wroute2_lingelu_lo_kernel(
                 x_scales[0, 4 * q : 4 * q + 4, :].bitcast(I32),
             )
         w_rows = w1.rearrange("(p j) n -> p j n", j=PACK)
-        x_rows = x_words[0].rearrange("p n r -> p (n r)").bitcast(I32)
-        nc.sync.dma_start(w_raw[0][:], w_rows[:, :, : N // 2])
-        nc.sync.dma_start(x_codes[:, :LEAD].bitcast(I32), x_rows[:, :LEAD])
+        for h in range(2):
+            nc.sync.dma_start(w_raw[h][:], w_rows[:, :, h * N // 2 : (h + 1) * N // 2])
+        nc.sync.dma_start(x_codes[:].bitcast(I32), x_words[0].rearrange("p n r -> p (n r)").bitcast(I32))
         nc.sync.dma_start(offsets[:], dst)
-        nc.sync.dma_start(gate_sb[:, :LEAD], gate[:, :LEAD])
-        nc.sync.dma_start(w_raw[1][:], w_rows[:, :, N // 2 :])
-        nc.sync.dma_start(x_codes[:, LEAD:].bitcast(I32), x_rows[:, LEAD:])
-        nc.sync.dma_start(gate_sb[:, LEAD:], gate[:, LEAD:])
+        nc.sync.dma_start(gate_sb[:], gate)
 
-        make_identity(nc, identity[:])
-        for t in range(2):
-            nc.vector.memset(windows[t][:], 0.0)
+        for t in range(PACK):
+            (nc.vector if t < 2 else nc.gpsimd).memset(windows[t][:], 0.0)
 
-        w_codes = [pool.tile([P, P], U32, name=f"w_codes{s}", align_bytes=64) for s in range(PACK)]
-        w_planes = [pool.tile([P, P], U8, name=f"w_plane{s}", align_bytes=64) for s in range(PACK)]
+        w_codes = [pool.tile([P, P], U32, name=f"w_codes{t}", align_bytes=64) for t in range(PACK)]
+        w_planes = [pool.tile([P, P], U8, name=f"w_plane{t}", align_bytes=64) for t in range(PACK)]
 
-        def round_weights(h, copy):
-            low = pool.tile([P, P * PACK], BF16, name=f"w_low{h}", tag=f"w_low{h}", align_bytes=64)
-            high = pool.tile([P, P * PACK], BF16, name=f"w_high{h}", tag=f"w_high{h}", align_bytes=64)
-            src = w_raw[h][:].rearrange("p j (l t) -> p l j t", t=PACK)
-            copy(low[:].rearrange("p (l t j) -> p l j t", t=2, j=PACK), src[:, :, :, :2])
-            dealt = high[:].rearrange("p (t l j) -> p l j t", t=2, j=PACK)
-            step = HALF if h == 0 else HALF // 2
-            for l0 in range(0, HALF, step):
-                copy(dealt[:, l0 : l0 + step], src[:, l0 : l0 + step, :, 2:])
-            return low, high
-
-        def quantize_weights(h, low, high):
-            nc.vector.quantize_mx(out=w_codes[h][:].bitcast(FP8X4), scales=w_planes[h][:], in_=low[:])
-            quantize_high(h, high)
-
-        def quantize_high(h, high):
+        def quantize_weights(h, t0, t1):
+            rounded = pool.tile([P, t1 - t0, HALF * PACK], BF16, name=f"w_rounded{h}_{t0}", align_bytes=64)
+            nc.vector.tensor_copy(
+                rounded[:].rearrange("p t (l j) -> p l j t", j=PACK),
+                w_raw[h][:].rearrange("p j (l t) -> p l j t", t=PACK)[:, :, :, t0:t1],
+            )
             cols = slice(h * HALF, (h + 1) * HALF)
-            for t in range(2):
+            for t in range(t0, t1):
                 nc.vector.quantize_mx(
-                    out=w_codes[2 + t][:, cols].bitcast(FP8X4),
-                    scales=w_planes[2 + t][:, cols],
-                    in_=high[:, t * HALF * PACK : (t + 1) * HALF * PACK],
+                    out=w_codes[t][:, cols].bitcast(FP8X4), scales=w_planes[t][:, cols], in_=rounded[:, t - t0, :]
                 )
 
-        def project(s, y, c0, c1, bank):
-            acc = psum.tile([P, c1 - c0], F32, name=f"acc{s}_{c0}", tag=f"bank{bank}")
-            nc.tensor.matmul_mx(
-                out=acc[:],
-                lhsT=w_codes[s][:].bitcast(FP8X4),
-                lhsT_scale=w_planes[s][:],
-                rhs=x_codes[:, c0:c1].bitcast(FP8X4),
-                rhs_scale=x_plane[:, c0:c1],
-                start=True,
-                stop=True,
-            )
-            nc.scalar.activation(y, acc[:], GELU)
+        quantize_weights(0, 0, PACK)
+        for t0, t1 in ((0, 1), (1, 2), (2, PACK)):
+            quantize_weights(1, t0, t1)
 
-        def scatter(s, y, c0, c1):
-            places = offsets[:, c0 // LIST_ROWS : c1 // LIST_ROWS]
-            nc.vector.tensor_tensor(windows[s][:].indirect(places), y, gate_sb[:, c0:c1], MULT)
+        def project(t, c0, c1, bank):
+            acc = psum.tile([P, c1 - c0], F32, name=f"acc{t}_{c0}", tag=f"bank{bank}")
+            step = c1 - c0 if c1 - c0 in (128, 256, 512) else P
+            for a in range(c0, c1, step):
+                nc.tensor.matmul_mx(
+                    out=acc[:, a - c0 : a - c0 + step],
+                    lhsT=w_codes[t][:].bitcast(FP8X4),
+                    lhsT_scale=w_planes[t][:],
+                    rhs=x_codes[:, a : a + step].bitcast(FP8X4),
+                    rhs_scale=x_plane[:, a : a + step],
+                    start=True,
+                    stop=True,
+                )
+            y = pool.tile([P, c1 - c0], F32, name=f"y{t}_{c0}", tag=f"y{t}_{c0}")
+            nc.scalar.activation(y[:], acc[:], GELU)
+            return y
 
-        first = w_raw[0][:].rearrange("p j (l t) -> p l j t", t=PACK)
-        lows = [
-            pool.tile([P, HALF * PACK], BF16, name=f"w_first{i}", tag=("w_high0", "w_low0")[i], align_bytes=64)
-            for i in range(2)
-        ]
-        for i, low in enumerate(lows):
-            words = slice(i * HALF // 2, (i + 1) * HALF // 2)
-            nc.vector.tensor_copy(low[:].rearrange("p (l t j) -> p l j t", t=2, j=PACK), first[:, words, :, :2])
-        for i, low in enumerate(lows):
-            cols = slice(i * HALF, (i + 1) * HALF)
-            nc.vector.quantize_mx(out=w_codes[0][:, cols].bitcast(FP8X4), scales=w_planes[0][:, cols], in_=low[:])
-        high = pool.tile([P, P * PACK], BF16, name="w_high0", tag="w_high0", align_bytes=64)
-        nc.vector.tensor_copy(high[:].rearrange("p (t l j) -> p l j t", t=2, j=PACK), first[:, :, :, 2:])
-        quantize_high(0, high)
-        windows.append(pool.tile([P, U], F32, name="window2", tag="w_high0", align_bytes=64))
-        nc.gpsimd.memset(windows[2][:], 0.0)
-        y_lead = pool.tile([P, LEAD], F32, name="y_lead", tag="y_lead")
-        for c0 in range(0, LEAD, P):
-            project(0, y_lead[:, c0 : c0 + P], c0, c0 + P, c0 // P)
-        scatter(0, y_lead[:], 0, LEAD)
+        def places(c0, c1):
+            return offsets[:, c0 // LIST_ROWS : c1 // LIST_ROWS]
 
-        quantize_weights(1, *round_weights(1, nc.scalar.copy))
-        y_rest = pool.tile([P, T - LEAD], F32, name="y_rest", tag="y_rest")
-        project(0, y_rest[:], LEAD, T, 2)
-        scatter(0, y_rest[:], LEAD, T)
-        ys = [pool.tile([P, T], F32, name=f"y{s}") for s in range(1, PACK)]
-        for c0 in range(0, T, T // 2):
-            project(1, ys[0][:, c0 : c0 + T // 2], c0, c0 + T // 2, 3 + c0 // (T // 2))
-        project(2, ys[1][:], 0, T, 5)
+        def gated(t, y):
+            g = pool.tile([P, T], F32, name=f"gated{t}")
+            nc.vector.tensor_tensor(g[:], y[:], gate_sb[:], MULT)
+            return g
 
-        gate_bank = psum.tile([P, T // P, P], F32, name="gate_bank", tag="bank7")
-        acc = psum.tile([P, T // P, P], F32, name="acc3", tag="bank6")
-        for c in range(T // P):
-            tokens = slice(c * P, (c + 1) * P)
-            nc.tensor.transpose(gate_bank[:, c, :], gate_sb[:, tokens], identity[:])
-        for c in range(T // P):
-            tokens = slice(c * P, (c + 1) * P)
-            nc.tensor.matmul_mx(
-                out=acc[:, c, :],
-                lhsT=x_codes[:, tokens].bitcast(FP8X4),
-                lhsT_scale=x_plane[:, tokens],
-                rhs=w_codes[3][:].bitcast(FP8X4),
-                rhs_scale=w_planes[3][:],
-                start=True,
-                stop=True,
-            )
-        gate_col = pool.tile([P, T // P], F32, name="gate_col")
-        nc.scalar.copy(gate_col[:], gate_bank[:, :, 0])
-        by_token = pool.tile([P, T // P, P], F32, name="by_token")
-        gated = pool.tile([P, T // P, P], F32, name="gated")
-        nc.scalar.activation(by_token[:], acc[:], GELU)
-        back = psum.tile([P, T // P, P], F32, name="back", tag="bank0")
-        for c in range(T // P):
-            nc.scalar.activation(gated[:, c, :], by_token[:, c, :], COPY, scale=gate_col[:, c : c + 1])
-            nc.tensor.transpose(back[:, c, :], gated[:, c, :], identity[:])
-        nc.scalar.copy(ys[2][:], back[:].rearrange("p c r -> p (c r)"))
-        windows.append(pool.tile([P, U], F32, name="window3", tag="y_rest"))
-        nc.gpsimd.memset(windows[3][:], 0.0)
+        def scatter_on_scalar(t, g):
+            for c0 in range(0, T, PIECE):
+                nc.scalar.activation(windows[t][:].indirect(places(c0, c0 + PIECE)), g[:, c0 : c0 + PIECE], COPY)
 
-        grouped = [pool.tile([P, (b - a) * PACK], BF16, name=f"grouped{a}", align_bytes=64) for a, b in CHUNKS]
-        turned = [pool.tile([P, TURN // P, 2, P], BF16, name=f"turned{k}") for k in range(U // TURN)]
         out_rows = out_0.rearrange("(l t) u -> l t u", t=PACK)
 
-        def turn_out(h):
-            for k in range(U // TURN):
-                bank = psum.tile([P, TURN // P, P], F32, name=f"turn{h}_{k}", tag=f"bank{3 + k}")
-                for j in range(TURN // P):
-                    u0 = k * TURN + j * P
-                    nc.tensor.transpose(bank[:, j, :], windows[h][:, u0 : u0 + P], identity[:])
-                nc.scalar.copy(turned[k][:, :, h, :], bank[:])
-
-        def turn_back():
-            for k in range(U // TURN):
-                bank = psum.tile([P, TURN], F32, name=f"back{k}", tag=f"bank{(7 + k) % 8}")
-                words = turned[k][:].rearrange("p j h r -> p j (h r)").bitcast(F32)
-                for j in range(TURN // P):
-                    nc.tensor.transpose(bank[:, j * P : (j + 1) * P], words[:, j, :], identity[:])
-                c = max(c for c, (a, b) in enumerate(CHUNKS) if a <= k * TURN)
-                a = k * TURN - CHUNKS[c][0]
-                target = grouped[c][:].bitcast(F32).rearrange("p (u e) -> p u e", e=2)[:, a : a + TURN, :]
-                nc.scalar.copy(target, bank[:].rearrange("p (u o) -> p u o", o=1).to_broadcast([P, TURN, 2]))
-
-        nc.sync.dma_start(out_rows[:HALF, :2, :], windows[0][:])
-        turn_out(0)
-        scatter(1, ys[0][:], 0, T)
-        nc.sync.dma_start(out_rows[HALF:, :2, :], windows[1][:])
-        turn_out(1)
-        turn_back()
-
-        def places(u0, u1):
-            c = max(c for c, (a, b) in enumerate(CHUNKS) if a <= u0)
-            a = CHUNKS[c][0]
-            return grouped[c][:].rearrange("p (u t) -> p u t", t=PACK)[:, u0 - a : u1 - a, :]
-
-        scatter(2, ys[1][:], 0, T)
+        y_lead = project(0, 0, LEAD, 0)
+        nc.vector.tensor_tensor(windows[0][:].indirect(places(0, LEAD)), y_lead[:], gate_sb[:, :LEAD], MULT)
+        g1 = gated(1, project(1, 0, T, 1))
+        y_rest = project(0, LEAD, T, 2)
+        nc.vector.tensor_tensor(windows[0][:].indirect(places(LEAD, T)), y_rest[:], gate_sb[:, LEAD:], MULT)
+        nc.sync.dma_start(out_rows[:, 0, :], windows[0][:])
+        g2 = gated(2, project(2, 0, T, 3))
+        g3 = gated(3, project(3, 0, T, 4))
+        scatter_on_scalar(1, g1)
+        nc.sync.dma_start(out_rows[:, 1, :], windows[1][:])
+        nc.vector.tensor_copy(windows[2][:].indirect(offsets[:]), g2[:])
         nc.sync.dma_start(out_rows[:, 2, :], windows[2][:])
-        both = windows[2][:, :VECTOR_PLACES].rearrange("p (u o) -> p u o", o=1).to_broadcast([P, VECTOR_PLACES, 2])
-        nc.gpsimd.tensor_scalar(places(0, VECTOR_PLACES)[:, :, 2:], both, 1.0, -0.0, MULT, ADD)
-        for a, b in CHUNKS[1:]:
-            nc.scalar.copy(places(a, b)[:, :, 2], windows[2][:, a:b])
-
-        nc.vector.tensor_copy(windows[3][:].indirect(offsets[:]), ys[2][:])
+        scatter_on_scalar(3, g3)
         nc.sync.dma_start(out_rows[:, 3, :], windows[3][:])
-        for a in range(0, U, 256):
-            copy = nc.vector.tensor_copy if a < VECTOR_PLACES else nc.scalar.copy
-            copy(places(a, a + 256)[:, :, 3], windows[3][:, a : a + 256])
+
+        tags = ("y2_0", "y3_0", "gate_sb", "pairs_last")
+        pairs = [pool.tile([P, 2, CHUNK, 2], BF16, name=f"pairs{c}", tag=tags[c]) for c in range(CHUNKS)]
+
+        def chunk_of(t, c):
+            return windows[t][:, c * CHUNK : (c + 1) * CHUNK]
+
+        for t in range(2):
+            for c in range(CHUNKS - 1):
+                nc.gpsimd.tensor_scalar(pairs[c][:, 0, :, t], chunk_of(t, c), 1.0, -0.0, MULT, ADD)
+        for t in range(2):
+            nc.vector.tensor_copy(pairs[CHUNKS - 1][:, 0, :, t], chunk_of(t, CHUNKS - 1))
+        for c in range(CHUNKS):
+            if c < CHUNKS // 2:
+                nc.vector.tensor_copy(pairs[c][:, 1, :, 0], chunk_of(2, c))
+            else:
+                both = chunk_of(2, c).rearrange("p (u o) -> p u o", o=1).to_broadcast([P, CHUNK, 2])
+                nc.vector.tensor_copy(pairs[c][:, 1, :, :], both)
+        for c in range(CHUNKS):
+            copy = nc.vector.tensor_copy if c < CHUNKS // 2 else nc.scalar.copy
+            copy(pairs[c][:, 1, :, 1], chunk_of(3, c))
+
+        grouped = [pool.tile([P, CHUNK * PACK], BF16, name=f"grouped{c}", align_bytes=64) for c in range(CHUNKS)]
+        for c in range(CHUNKS):
+            copy, word = (nc.vector.tensor_copy, I32) if c < CHUNKS // 2 else (nc.scalar.copy, U32)
+            words = pairs[c][:].rearrange("p e u o -> p e (u o)").bitcast(word)
+            copy(grouped[c][:].bitcast(word).rearrange("p (u e) -> p u e", e=2), words.rearrange("p e u -> p u e"))
 
         o_plane = pool.tile([P, U], U8, name="o_plane", align_bytes=64)
         words_out = out_1[0].rearrange("p u r -> p (u r)").bitcast(I32)
-        for c, a in ((0, 0), (0, 256), (1, 512), (2, 768)):
-            b = a + 256
-            codes = pool.tile([P, b - a], U32, name=f"o_codes{a}", align_bytes=64)
-            nc.vector.quantize_mx(
-                out=codes[:].bitcast(FP8X4),
-                scales=o_plane[:, a:b],
-                in_=grouped[c][:, (a - CHUNKS[c][0]) * PACK : (b - CHUNKS[c][0]) * PACK],
-            )
-            nc.sync.dma_start(words_out[:, a:b], codes[:].bitcast(I32))
+        for c in range(CHUNKS):
+            cols = slice(c * CHUNK, (c + 1) * CHUNK)
+            codes = pool.tile([P, CHUNK], U32, name=f"o_codes{c}", align_bytes=64)
+            nc.vector.quantize_mx(out=codes[:].bitcast(FP8X4), scales=o_plane[:, cols], in_=grouped[c][:])
+            nc.sync.dma_start(words_out[:, cols], codes[:].bitcast(I32))
         for q in range(QUADRANTS):
             queue = nc.scalar if q < 1 else nc.sync
             queue.dma_start(

@@ -98,13 +98,12 @@ def tile_picked_wroute2_lingelu_lo_kernel(
             return offsets[:, c0 // LIST_ROWS : c1 // LIST_ROWS]
 
         def gated(t, y):
-            g = pool.tile([P, T], F32, name=f"gated{t}")
+            g = pool.tile([P, T], F32, name=f"gated{t}", tag=f"gated{t}")
             nc.vector.tensor_tensor(g[:], y[:], gate_sb[:], MULT)
             return g
 
-        def scatter_on_scalar(t, g):
-            for c0 in range(0, T, PIECE):
-                nc.scalar.activation(windows[t][:].indirect(places(c0, c0 + PIECE)), g[:, c0 : c0 + PIECE], COPY)
+        def scatter_on_scalar(t, g, c0):
+            nc.scalar.activation(windows[t][:].indirect(places(c0, c0 + PIECE)), g[:, c0 : c0 + PIECE], COPY)
 
         out_rows = out_0.rearrange("(l t) u -> l t u", t=PACK)
 
@@ -114,26 +113,29 @@ def tile_picked_wroute2_lingelu_lo_kernel(
         y_rest = project(0, LEAD, T, 2)
         nc.vector.tensor_tensor(windows[0][:].indirect(places(LEAD, T)), y_rest[:], gate_sb[:, LEAD:], MULT)
         nc.sync.dma_start(out_rows[:, 0, :], windows[0][:])
-        g2 = gated(2, project(2, 0, T, 3))
         g3 = gated(3, project(3, 0, T, 4))
-        scatter_on_scalar(1, g1)
+        y2 = project(2, 0, T, 3)
+        for c0 in range(0, T, PIECE):
+            scatter_on_scalar(1, g1, c0)
         nc.sync.dma_start(out_rows[:, 1, :], windows[1][:])
-        nc.vector.tensor_copy(windows[2][:].indirect(offsets[:]), g2[:])
+        nc.vector.tensor_tensor(windows[2][:].indirect(offsets[:]), y2[:], gate_sb[:], MULT)
         nc.sync.dma_start(out_rows[:, 2, :], windows[2][:])
-        scatter_on_scalar(3, g3)
-        nc.sync.dma_start(out_rows[:, 3, :], windows[3][:])
 
-        tags = ("y2_0", "y3_0", "gate_sb", "pairs_last")
+        tags = ("gate_sb", "y2_0", "pairs2", "gated1")
         pairs = [pool.tile([P, 2, CHUNK, 2], BF16, name=f"pairs{c}", tag=tags[c]) for c in range(CHUNKS)]
 
         def chunk_of(t, c):
             return windows[t][:, c * CHUNK : (c + 1) * CHUNK]
 
+        scatter_on_scalar(3, g3, 0)
+        for t in range(2):
+            nc.scalar.copy(pairs[CHUNKS - 1][:, 0, :, t], chunk_of(t, CHUNKS - 1))
+        scatter_on_scalar(3, g3, PIECE)
+        nc.sync.dma_start(out_rows[:, 3, :], windows[3][:])
+
         for t in range(2):
             for c in range(CHUNKS - 1):
-                nc.gpsimd.tensor_scalar(pairs[c][:, 0, :, t], chunk_of(t, c), 1.0, -0.0, MULT, ADD)
-        for t in range(2):
-            nc.vector.tensor_copy(pairs[CHUNKS - 1][:, 0, :, t], chunk_of(t, CHUNKS - 1))
+                nc.vector.tensor_copy(pairs[c][:, 0, :, t], chunk_of(t, c))
         for c in range(CHUNKS):
             if c < CHUNKS // 2:
                 nc.vector.tensor_copy(pairs[c][:, 1, :, 0], chunk_of(2, c))

@@ -15,7 +15,6 @@ FP8X4 = mybir.dt.float8_e4m3fn_x4
 GELU = mybir.ActivationFunctionType.Gelu_apprx_tanh
 COPY = mybir.ActivationFunctionType.Copy
 MULT = mybir.AluOpType.mult
-ADD = mybir.AluOpType.add
 
 P = 128
 PACK = 4
@@ -23,9 +22,11 @@ QUADRANTS = 4
 LIST_ROWS = 16
 HALF = P // 2
 LEAD = 128
-PIECE = T // 2
-CHUNK = 256
-CHUNKS = U // CHUNK
+LINE = 4
+LONG = 384
+CHUNKS = ((0, 256), (256, 512), (512, 896), (896, 1024))
+VECTOR_PIECES = ((0, 256), (256, 608))
+SCALAR_PIECES = ((608, 896), (896, 1024))
 
 
 def tile_picked_wroute2_lingelu_lo_kernel(
@@ -62,7 +63,7 @@ def tile_picked_wroute2_lingelu_lo_kernel(
         w_planes = [pool.tile([P, P], U8, name=f"w_plane{t}", align_bytes=64) for t in range(PACK)]
 
         def quantize_weights(h, t0, t1):
-            rounded = pool.tile([P, t1 - t0, HALF * PACK], BF16, name=f"w_rounded{h}_{t0}", align_bytes=64)
+            rounded = pool.tile([P, t1 - t0, HALF * PACK], BF16, name=f"w_rounded{h}_{t0}", tag=f"w_rounded{h}_{t0 % 2}", align_bytes=64)
             nc.vector.tensor_copy(
                 rounded[:].rearrange("p t (l j) -> p l j t", j=PACK),
                 w_raw[h][:].rearrange("p j (l t) -> p l j t", t=PACK)[:, :, :, t0:t1],
@@ -77,7 +78,7 @@ def tile_picked_wroute2_lingelu_lo_kernel(
         for t0, t1 in ((0, 1), (1, 2), (2, PACK)):
             quantize_weights(1, t0, t1)
 
-        def project(t, c0, c1, bank):
+        def project(t, c0, c1, bank, y=None):
             acc = psum.tile([P, c1 - c0], F32, name=f"acc{t}_{c0}", tag=f"bank{bank}")
             step = c1 - c0 if c1 - c0 in (128, 256, 512) else P
             for a in range(c0, c1, step):
@@ -90,75 +91,76 @@ def tile_picked_wroute2_lingelu_lo_kernel(
                     start=True,
                     stop=True,
                 )
-            y = pool.tile([P, c1 - c0], F32, name=f"y{t}_{c0}", tag=f"y{t}_{c0}")
-            nc.scalar.activation(y[:], acc[:], GELU)
+            if y is None:
+                y = pool.tile([P, c1 - c0], F32, name=f"y{t}_{c0}")[:]
+            nc.scalar.activation(y, acc[:], GELU)
             return y
 
         def places(c0, c1):
             return offsets[:, c0 // LIST_ROWS : c1 // LIST_ROWS]
 
-        def gated(t, y):
-            g = pool.tile([P, T], F32, name=f"gated{t}", tag=f"gated{t}")
-            nc.vector.tensor_tensor(g[:], y[:], gate_sb[:], MULT)
-            return g
-
-        def scatter_on_scalar(t, g, c0):
-            nc.scalar.activation(windows[t][:].indirect(places(c0, c0 + PIECE)), g[:, c0 : c0 + PIECE], COPY)
-
         out_rows = out_0.rearrange("(l t) u -> l t u", t=PACK)
 
-        y_lead = project(0, 0, LEAD, 0)
-        nc.vector.tensor_tensor(windows[0][:].indirect(places(0, LEAD)), y_lead[:], gate_sb[:, :LEAD], MULT)
-        g1 = gated(1, project(1, 0, T, 1))
-        y_rest = project(0, LEAD, T, 2)
-        nc.vector.tensor_tensor(windows[0][:].indirect(places(LEAD, T)), y_rest[:], gate_sb[:, LEAD:], MULT)
+        staged = pool.tile([P, PACK, U], F32, name="staged")
+
+        def fused_scatter(t, y, c0, c1):
+            nc.vector.tensor_tensor(windows[t][:].indirect(places(c0, c1)), y, gate_sb[:, c0:c1], MULT)
+
+        def gated(t, y, c0, c1):
+            g = pool.tile([P, c1 - c0], F32, name=f"gated{t}_{c0}")
+            nc.vector.tensor_tensor(g[:], y[:], gate_sb[:, c0:c1], MULT)
+            return g
+
+        def copy_scatter(t, g, c0, c1):
+            nc.scalar.activation(windows[t][:].indirect(places(c0, c1)), g, COPY)
+
+        y0_lead = project(0, 0, LEAD, 0)
+        fused_scatter(0, y0_lead[:], 0, LEAD)
+        y1 = pool.tile([P, T], F32, name="y1")
+        for half, bank in ((0, 1), (1, 6)):
+            project(1, half * T // 2, (half + 1) * T // 2, bank, y1[:, half * T // 2 : (half + 1) * T // 2])
+        g1 = gated(1, y1, 0, T)
+        g3_lead = gated(3, project(3, 0, T - LONG, 5), 0, T - LONG)
+        y0_rest = project(0, LEAD, T, 2)
+        fused_scatter(0, y0_rest[:], LEAD, T)
+        nc.sync.dma_start(staged[:, 0, :], windows[0][:])
         nc.sync.dma_start(out_rows[:, 0, :], windows[0][:])
-        g3 = gated(3, project(3, 0, T, 4))
-        y2 = project(2, 0, T, 3)
-        for c0 in range(0, T, PIECE):
-            scatter_on_scalar(1, g1, c0)
+        g3_rest = gated(3, project(3, T - LONG, T, 3), T - LONG, T)
+        y2 = project(2, 0, T, 4)
+        copy_scatter(1, g1[:, :LONG], 0, LONG)
+        copy_scatter(3, g3_lead[:], 0, T - LONG)
+        copy_scatter(1, g1[:, LONG:], LONG, T)
         nc.sync.dma_start(out_rows[:, 1, :], windows[1][:])
-        nc.vector.tensor_tensor(windows[2][:].indirect(offsets[:]), y2[:], gate_sb[:], MULT)
+        fused_scatter(2, y2[:], 0, T)
         nc.sync.dma_start(out_rows[:, 2, :], windows[2][:])
-
-        tags = ("gate_sb", "y2_0", "pairs2", "gated1")
-        pairs = [pool.tile([P, 2, CHUNK, 2], BF16, name=f"pairs{c}", tag=tags[c]) for c in range(CHUNKS)]
-
-        def chunk_of(t, c):
-            return windows[t][:, c * CHUNK : (c + 1) * CHUNK]
-
-        scatter_on_scalar(3, g3, 0)
-        for t in range(2):
-            nc.scalar.copy(pairs[CHUNKS - 1][:, 0, :, t], chunk_of(t, CHUNKS - 1))
-        scatter_on_scalar(3, g3, PIECE)
+        for t in (1, 2):
+            nc.vector.tensor_copy(staged[:, t, :], windows[t][:])
+        copy_scatter(3, g3_rest[:], T - LONG, T)
         nc.sync.dma_start(out_rows[:, 3, :], windows[3][:])
 
-        for t in range(2):
-            for c in range(CHUNKS - 1):
-                nc.vector.tensor_copy(pairs[c][:, 0, :, t], chunk_of(t, c))
-        for c in range(CHUNKS):
-            if c < CHUNKS // 2:
-                nc.vector.tensor_copy(pairs[c][:, 1, :, 0], chunk_of(2, c))
-            else:
-                both = chunk_of(2, c).rearrange("p (u o) -> p u o", o=1).to_broadcast([P, CHUNK, 2])
-                nc.vector.tensor_copy(pairs[c][:, 1, :, :], both)
-        for c in range(CHUNKS):
-            copy = nc.vector.tensor_copy if c < CHUNKS // 2 else nc.scalar.copy
-            copy(pairs[c][:, 1, :, 1], chunk_of(3, c))
-
-        grouped = [pool.tile([P, CHUNK * PACK], BF16, name=f"grouped{c}", align_bytes=64) for c in range(CHUNKS)]
-        for c in range(CHUNKS):
-            copy, word = (nc.vector.tensor_copy, I32) if c < CHUNKS // 2 else (nc.scalar.copy, U32)
-            words = pairs[c][:].rearrange("p e u o -> p e (u o)").bitcast(word)
-            copy(grouped[c][:].bitcast(word).rearrange("p (u e) -> p u e", e=2), words.rearrange("p e u -> p u e"))
+        grouped = [pool.tile([P, (b - a) * PACK], BF16, name=f"grouped{a}", align_bytes=64) for a, b in CHUNKS]
+        shares = ((nc.vector.tensor_copy, VECTOR_PIECES), (nc.scalar.copy, SCALAR_PIECES))
+        for copy, pieces in shares:
+            for a, b in pieces:
+                copy(staged[:, 3, a:b], windows[3][:, a:b])
+        for copy, pieces in shares:
+            for a, b in pieces:
+                for tile, (c0, c1) in zip(grouped, CHUNKS):
+                    u0, u1 = max(a, c0), min(b, c1)
+                    if u0 >= u1:
+                        continue
+                    target = tile[:, (u0 - c0) * PACK : (u1 - c0) * PACK]
+                    copy(
+                        target.rearrange("p (g i t) -> p g t i", i=LINE, t=PACK),
+                        staged[:, :, u0:u1].rearrange("p t (g i) -> p g t i", i=LINE),
+                    )
 
         o_plane = pool.tile([P, U], U8, name="o_plane", align_bytes=64)
         words_out = out_1[0].rearrange("p u r -> p (u r)").bitcast(I32)
-        for c in range(CHUNKS):
-            cols = slice(c * CHUNK, (c + 1) * CHUNK)
-            codes = pool.tile([P, CHUNK], U32, name=f"o_codes{c}", align_bytes=64)
-            nc.vector.quantize_mx(out=codes[:].bitcast(FP8X4), scales=o_plane[:, cols], in_=grouped[c][:])
-            nc.sync.dma_start(words_out[:, cols], codes[:].bitcast(I32))
+        for tile, (c0, c1) in zip(grouped, CHUNKS):
+            codes = pool.tile([P, c1 - c0], U32, name=f"o_codes{c0}", align_bytes=64)
+            nc.vector.quantize_mx(out=codes[:].bitcast(FP8X4), scales=o_plane[:, c0:c1], in_=tile[:])
+            nc.sync.dma_start(words_out[:, c0:c1], codes[:].bitcast(I32))
         for q in range(QUADRANTS):
             queue = nc.scalar if q < 1 else nc.sync
             queue.dma_start(

@@ -15,6 +15,7 @@ FP8X4 = mybir.dt.float8_e4m3fn_x4
 GELU = mybir.ActivationFunctionType.Gelu_apprx_tanh
 COPY = mybir.ActivationFunctionType.Copy
 MULT = mybir.AluOpType.mult
+ADD = mybir.AluOpType.add
 
 P = 128
 PACK = 4
@@ -23,7 +24,6 @@ LIST_ROWS = 16
 HALF = P // 2
 LEAD = 128
 LINE = 4
-LONG = 384
 CHUNKS = ((0, 256), (256, 512), (512, 896), (896, 1024))
 VECTOR_PIECES = ((0, 256), (256, 608))
 SCALAR_PIECES = ((608, 896), (896, 1024))
@@ -63,7 +63,7 @@ def tile_picked_wroute2_lingelu_lo_kernel(
         w_planes = [pool.tile([P, P], U8, name=f"w_plane{t}", align_bytes=64) for t in range(PACK)]
 
         def quantize_weights(h, t0, t1):
-            rounded = pool.tile([P, t1 - t0, HALF * PACK], BF16, name=f"w_rounded{h}_{t0}", tag=f"w_rounded{h}_{t0 % 2}", align_bytes=64)
+            rounded = pool.tile([P, t1 - t0, HALF * PACK], BF16, name=f"w_rounded{h}_{t0}", align_bytes=64)
             nc.vector.tensor_copy(
                 rounded[:].rearrange("p t (l j) -> p l j t", j=PACK),
                 w_raw[h][:].rearrange("p j (l t) -> p l j t", t=PACK)[:, :, :, t0:t1],
@@ -75,10 +75,10 @@ def tile_picked_wroute2_lingelu_lo_kernel(
                 )
 
         quantize_weights(0, 0, PACK)
-        for t0, t1 in ((0, 1), (1, 2), (2, PACK)):
+        for t0, t1 in ((0, 2), (2, PACK)):
             quantize_weights(1, t0, t1)
 
-        def project(t, c0, c1, bank, y=None):
+        def project(t, c0, c1, bank):
             acc = psum.tile([P, c1 - c0], F32, name=f"acc{t}_{c0}", tag=f"bank{bank}")
             step = c1 - c0 if c1 - c0 in (128, 256, 512) else P
             for a in range(c0, c1, step):
@@ -91,10 +91,9 @@ def tile_picked_wroute2_lingelu_lo_kernel(
                     start=True,
                     stop=True,
                 )
-            if y is None:
-                y = pool.tile([P, c1 - c0], F32, name=f"y{t}_{c0}")[:]
-            nc.scalar.activation(y, acc[:], GELU)
-            return y
+            y = pool.tile([P, c1 - c0], F32, name=f"y{t}_{c0}")
+            nc.scalar.activation(y[:], acc[:], GELU)
+            return y[:]
 
         def places(c0, c1):
             return offsets[:, c0 // LIST_ROWS : c1 // LIST_ROWS]
@@ -103,46 +102,43 @@ def tile_picked_wroute2_lingelu_lo_kernel(
 
         staged = pool.tile([P, PACK, U], F32, name="staged")
 
-        def fused_scatter(t, y, c0, c1):
-            nc.vector.tensor_tensor(windows[t][:].indirect(places(c0, c1)), y, gate_sb[:, c0:c1], MULT)
-
-        def gated(t, y, c0, c1):
+        def gated(engine, t, c0, c1, bank):
+            y = project(t, c0, c1, bank)
             g = pool.tile([P, c1 - c0], F32, name=f"gated{t}_{c0}")
-            nc.vector.tensor_tensor(g[:], y[:], gate_sb[:, c0:c1], MULT)
+            engine.tensor_tensor(g[:], y, gate_sb[:, c0:c1], MULT)
             return g
 
-        def copy_scatter(t, g, c0, c1):
-            nc.scalar.activation(windows[t][:].indirect(places(c0, c1)), g, COPY)
+        def vector_scatter(t, g, c0, c1):
+            nc.vector.tensor_copy(windows[t][:].indirect(places(c0, c1)), g[:])
 
-        y0_lead = project(0, 0, LEAD, 0)
-        fused_scatter(0, y0_lead[:], 0, LEAD)
-        y1 = pool.tile([P, T], F32, name="y1")
-        for half, bank in ((0, 1), (1, 6)):
-            project(1, half * T // 2, (half + 1) * T // 2, bank, y1[:, half * T // 2 : (half + 1) * T // 2])
-        g1 = gated(1, y1, 0, T)
-        g3_lead = gated(3, project(3, 0, T - LONG, 5), 0, T - LONG)
-        y0_rest = project(0, LEAD, T, 2)
-        fused_scatter(0, y0_rest[:], LEAD, T)
+        def scalar_scatter(t, g, c0, c1):
+            nc.scalar.activation(windows[t][:].indirect(places(c0, c1)), g[:], COPY)
+
+        leads = [gated(nc.vector, t, 0, LEAD, t) for t in range(2)]
+        g3_lead = gated(nc.gpsimd, 3, 0, LEAD, 3)
+        for t in range(2):
+            vector_scatter(t, leads[t], 0, LEAD)
+        vector_scatter(0, gated(nc.gpsimd, 0, LEAD, T, 2), LEAD, T)
         nc.sync.dma_start(staged[:, 0, :], windows[0][:])
         nc.sync.dma_start(out_rows[:, 0, :], windows[0][:])
-        g3_rest = gated(3, project(3, T - LONG, T, 3), T - LONG, T)
-        y2 = project(2, 0, T, 4)
-        copy_scatter(1, g1[:, :LONG], 0, LONG)
-        copy_scatter(3, g3_lead[:], 0, T - LONG)
-        copy_scatter(1, g1[:, LONG:], LONG, T)
+        g1_rest = gated(nc.gpsimd, 1, LEAD, T, 4)
+        g2 = gated(nc.gpsimd, 2, 0, T, 5)
+        g3_rest = gated(nc.gpsimd, 3, LEAD, T, 6)
+        scalar_scatter(3, g3_lead, 0, LEAD)
+        scalar_scatter(1, g1_rest, LEAD, T)
         nc.sync.dma_start(out_rows[:, 1, :], windows[1][:])
-        fused_scatter(2, y2[:], 0, T)
+        nc.gpsimd.tensor_scalar(staged[:, 1, :], windows[1][:], 1.0, -0.0, MULT, ADD)
+        vector_scatter(2, g2, 0, T)
         nc.sync.dma_start(out_rows[:, 2, :], windows[2][:])
-        for t in (1, 2):
-            nc.vector.tensor_copy(staged[:, t, :], windows[t][:])
-        copy_scatter(3, g3_rest[:], T - LONG, T)
+        scalar_scatter(3, g3_rest, LEAD, T)
         nc.sync.dma_start(out_rows[:, 3, :], windows[3][:])
 
         grouped = [pool.tile([P, (b - a) * PACK], BF16, name=f"grouped{a}", align_bytes=64) for a, b in CHUNKS]
         shares = ((nc.vector.tensor_copy, VECTOR_PIECES), (nc.scalar.copy, SCALAR_PIECES))
-        for copy, pieces in shares:
-            for a, b in pieces:
-                copy(staged[:, 3, a:b], windows[3][:, a:b])
+        for t in (2, 3):
+            for copy, pieces in shares:
+                a, b = pieces[0][0], pieces[-1][1]
+                copy(staged[:, t, a:b], windows[t][:, a:b])
         for copy, pieces in shares:
             for a, b in pieces:
                 for tile, (c0, c1) in zip(grouped, CHUNKS):

@@ -42,7 +42,7 @@ def tile_picked_wroute2_lingelu_lo_kernel(
         x_plane = pool.tile([P, T], U8, name="x_plane", align_bytes=64)
         gate_sb = pool.tile([P, T], F32, name="gate_sb", tag="gate_sb")
         w_raw = [pool.tile([P, PACK, N // 2], F32, name=f"w_raw{h}") for h in range(2)]
-        windows = [pool.tile([P, U], F32, name=f"window{t}") for t in range(PACK)]
+        windows = [pool.tile([P, U], F32, name=f"window{t}") for t in range(PACK - 1)]
 
         for q in range(QUADRANTS):
             nc.scalar.dma_start(
@@ -56,14 +56,14 @@ def tile_picked_wroute2_lingelu_lo_kernel(
         nc.sync.dma_start(offsets[:], dst)
         nc.sync.dma_start(gate_sb[:], gate)
 
-        for t in range(PACK):
+        for t in range(PACK - 1):
             (nc.vector if t < 2 else nc.gpsimd).memset(windows[t][:], 0.0)
 
         w_codes = [pool.tile([P, P], U32, name=f"w_codes{t}", align_bytes=64) for t in range(PACK)]
         w_planes = [pool.tile([P, P], U8, name=f"w_plane{t}", align_bytes=64) for t in range(PACK)]
 
         def quantize_weights(h, t0, t1):
-            rounded = pool.tile([P, t1 - t0, HALF * PACK], BF16, name=f"w_rounded{h}_{t0}", align_bytes=64)
+            rounded = pool.tile([P, t1 - t0, HALF * PACK], BF16, name=f"w_rounded{h}_{t0}", tag=f"w_rounded{h}_{t0}", align_bytes=64)
             nc.vector.tensor_copy(
                 rounded[:].rearrange("p t (l j) -> p l j t", j=PACK),
                 w_raw[h][:].rearrange("p j (l t) -> p l j t", t=PACK)[:, :, :, t0:t1],
@@ -77,6 +77,8 @@ def tile_picked_wroute2_lingelu_lo_kernel(
         quantize_weights(0, 0, PACK)
         for t0, t1 in ((0, 2), (2, PACK)):
             quantize_weights(1, t0, t1)
+        windows.append(pool.tile([P, U], F32, name="window3", tag="w_rounded1_2", align_bytes=64))
+        nc.gpsimd.memset(windows[3][:], 0.0)
 
         def project(t, c0, c1, bank):
             acc = psum.tile([P, c1 - c0], F32, name=f"acc{t}_{c0}", tag=f"bank{bank}")

@@ -24,9 +24,9 @@ LIST_ROWS = 16
 HALF = P // 2
 LEAD = 128
 LINE = 4
-CHUNKS = ((0, 256), (256, 512), (512, 896), (896, 1024))
-VECTOR_PIECES = ((0, 256), (256, 608))
-SCALAR_PIECES = ((608, 896), (896, 1024))
+CHUNKS = ((0, 256), (256, 640), (640, 896), (896, 1024))
+VECTOR_PIECES = ((0, 256), (256, 640))
+SCALAR_PIECES = ((640, 896), (896, 1024))
 
 
 def tile_picked_wroute2_lingelu_lo_kernel(
@@ -137,10 +137,11 @@ def tile_picked_wroute2_lingelu_lo_kernel(
 
         grouped = [pool.tile([P, (b - a) * PACK], BF16, name=f"grouped{a}", align_bytes=64) for a, b in CHUNKS]
         shares = ((nc.vector.tensor_copy, VECTOR_PIECES), (nc.scalar.copy, SCALAR_PIECES))
-        for t in (2, 3):
-            for copy, pieces in shares:
-                a, b = pieces[0][0], pieces[-1][1]
-                copy(staged[:, t, a:b], windows[t][:, a:b])
+        for copy, pieces in shares:
+            a, b = pieces[0][0], pieces[-1][1]
+            copy(staged[:, 2, a:b], windows[2][:, a:b])
+            for a, b in pieces:
+                copy(staged[:, 3, a:b], windows[3][:, a:b])
         for copy, pieces in shares:
             for a, b in pieces:
                 for tile, (c0, c1) in zip(grouped, CHUNKS):

@@ -24,6 +24,9 @@ LIST_ROWS = 16
 HALF = P // 2
 LEAD = 128
 LINE = 4
+WIDTHS = (64, 128, 256, 512)
+SHARE = 160
+SHARE_PROJECTED = 192
 CHUNKS = ((0, 256), (256, 640), (640, 896), (896, 1024))
 VECTOR_PIECES = ((0, 256), (256, 640))
 SCALAR_PIECES = ((640, 896), (896, 1024))
@@ -80,10 +83,11 @@ def tile_picked_wroute2_lingelu_lo_kernel(
         windows.append(pool.tile([P, U], F32, name="window3", tag="w_rounded1_2", align_bytes=64))
         nc.gpsimd.memset(windows[3][:], 0.0)
 
-        def project(t, c0, c1, bank):
+        def project(t, c0, c1, bank, y):
             acc = psum.tile([P, c1 - c0], F32, name=f"acc{t}_{c0}", tag=f"bank{bank}")
-            step = c1 - c0 if c1 - c0 in (128, 256, 512) else P
-            for a in range(c0, c1, step):
+            a = c0
+            while a < c1:
+                step = max(n for n in WIDTHS if n <= c1 - a)
                 nc.tensor.matmul_mx(
                     out=acc[:, a - c0 : a - c0 + step],
                     lhsT=w_codes[t][:].bitcast(FP8X4),
@@ -93,9 +97,8 @@ def tile_picked_wroute2_lingelu_lo_kernel(
                     start=True,
                     stop=True,
                 )
-            y = pool.tile([P, c1 - c0], F32, name=f"y{t}_{c0}")
-            nc.scalar.activation(y[:], acc[:], GELU)
-            return y[:]
+                a = a + step
+            nc.scalar.activation(y, acc[:], GELU)
 
         def places(c0, c1):
             return offsets[:, c0 // LIST_ROWS : c1 // LIST_ROWS]
@@ -104,11 +107,15 @@ def tile_picked_wroute2_lingelu_lo_kernel(
 
         staged = pool.tile([P, PACK, U], F32, name="staged")
 
-        def gated(engine, t, c0, c1, bank):
-            y = project(t, c0, c1, bank)
+        def times_gate(engine, t, y, c0, c1):
             g = pool.tile([P, c1 - c0], F32, name=f"gated{t}_{c0}")
             engine.tensor_tensor(g[:], y, gate_sb[:, c0:c1], MULT)
             return g
+
+        def gated(engine, t, c0, c1, bank):
+            y = pool.tile([P, c1 - c0], F32, name=f"y{t}_{c0}")
+            project(t, c0, c1, bank, y[:])
+            return times_gate(engine, t, y[:], c0, c1)
 
         def vector_scatter(t, g, c0, c1):
             nc.vector.tensor_copy(windows[t][:].indirect(places(c0, c1)), g[:])
@@ -116,18 +123,22 @@ def tile_picked_wroute2_lingelu_lo_kernel(
         def scalar_scatter(t, g, c0, c1):
             nc.scalar.activation(windows[t][:].indirect(places(c0, c1)), g[:], COPY)
 
-        leads = [gated(nc.vector, t, 0, LEAD, t) for t in range(2)]
+        g0_lead = gated(nc.vector, 0, 0, LEAD, 0)
+        y1 = pool.tile([P, T], F32, name="y1")
+        project(1, 0, SHARE_PROJECTED, 1, y1[:, :SHARE_PROJECTED])
+        g1_lead = times_gate(nc.vector, 1, y1[:, :SHARE], 0, SHARE)
         g3_lead = gated(nc.gpsimd, 3, 0, LEAD, 3)
-        for t in range(2):
-            vector_scatter(t, leads[t], 0, LEAD)
+        vector_scatter(0, g0_lead, 0, LEAD)
+        vector_scatter(1, g1_lead, 0, SHARE)
         vector_scatter(0, gated(nc.gpsimd, 0, LEAD, T, 2), LEAD, T)
         nc.sync.dma_start(staged[:, 0, :], windows[0][:])
         nc.sync.dma_start(out_rows[:, 0, :], windows[0][:])
-        g1_rest = gated(nc.gpsimd, 1, LEAD, T, 4)
+        project(1, SHARE_PROJECTED, T, 4, y1[:, SHARE_PROJECTED:])
+        g1_rest = times_gate(nc.gpsimd, 1, y1[:, SHARE:], SHARE, T)
         g2 = gated(nc.gpsimd, 2, 0, T, 5)
         g3_rest = gated(nc.gpsimd, 3, LEAD, T, 6)
         scalar_scatter(3, g3_lead, 0, LEAD)
-        scalar_scatter(1, g1_rest, LEAD, T)
+        scalar_scatter(1, g1_rest, SHARE, T)
         nc.sync.dma_start(out_rows[:, 1, :], windows[1][:])
         nc.gpsimd.tensor_scalar(staged[:, 1, :], windows[1][:], 1.0, -0.0, MULT, ADD)
         vector_scatter(2, g2, 0, T)

@@ -22,14 +22,14 @@ PACK = 4
 QUADRANTS = 4
 LIST_ROWS = 16
 HALF = P // 2
-LEAD = 128
 LINE = 4
-WIDTHS = (64, 128, 256, 512)
-SHARE = 160
-SHARE_PROJECTED = 192
+WIDTHS = (128, 256, 512)
+LEAD = 128
+SHARE = 128
+DMA_STAGED = 512
 CHUNKS = ((0, 256), (256, 640), (640, 896), (896, 1024))
-VECTOR_PIECES = ((0, 256), (256, 640))
-SCALAR_PIECES = ((640, 896), (896, 1024))
+VECTOR_PIECES = ((0, 256), (256, 544))
+SCALAR_PIECES = ((544, 640), (640, 896), (896, 1024))
 
 
 def tile_picked_wroute2_lingelu_lo_kernel(
@@ -43,7 +43,7 @@ def tile_picked_wroute2_lingelu_lo_kernel(
         offsets = pool.tile([P, T // LIST_ROWS], U16, name="offsets")
         x_codes = pool.tile([P, T], U32, name="x_codes", align_bytes=64)
         x_plane = pool.tile([P, T], U8, name="x_plane", align_bytes=64)
-        gate_sb = pool.tile([P, T], F32, name="gate_sb", tag="gate_sb")
+        gate_sb = pool.tile([P, T], F32, name="gate_sb")
         w_raw = [pool.tile([P, PACK, N // 2], F32, name=f"w_raw{h}") for h in range(2)]
         windows = [pool.tile([P, U], F32, name=f"window{t}") for t in range(PACK - 1)]
 
@@ -83,7 +83,9 @@ def tile_picked_wroute2_lingelu_lo_kernel(
         windows.append(pool.tile([P, U], F32, name="window3", tag="w_rounded1_2", align_bytes=64))
         nc.gpsimd.memset(windows[3][:], 0.0)
 
-        def project(t, c0, c1, bank, y):
+        y = [pool.tile([P, T], F32, name=f"y{t}") for t in range(PACK)]
+
+        def project(t, c0, c1, bank):
             acc = psum.tile([P, c1 - c0], F32, name=f"acc{t}_{c0}", tag=f"bank{bank}")
             a = c0
             while a < c1:
@@ -98,72 +100,67 @@ def tile_picked_wroute2_lingelu_lo_kernel(
                     stop=True,
                 )
                 a = a + step
-            nc.scalar.activation(y, acc[:], GELU)
+            nc.scalar.activation(y[t][:, c0:c1], acc[:], GELU)
 
-        def places(c0, c1):
-            return offsets[:, c0 // LIST_ROWS : c1 // LIST_ROWS]
-
-        out_rows = out_0.rearrange("(l t) u -> l t u", t=PACK)
-
-        staged = pool.tile([P, PACK, U], F32, name="staged")
-
-        def times_gate(engine, t, y, c0, c1):
+        def times_gate(engine, t, c0, c1):
             g = pool.tile([P, c1 - c0], F32, name=f"gated{t}_{c0}")
-            engine.tensor_tensor(g[:], y, gate_sb[:, c0:c1], MULT)
+            engine.tensor_tensor(g[:], y[t][:, c0:c1], gate_sb[:, c0:c1], MULT)
             return g
 
-        def gated(engine, t, c0, c1, bank):
-            y = pool.tile([P, c1 - c0], F32, name=f"y{t}_{c0}")
-            project(t, c0, c1, bank, y[:])
-            return times_gate(engine, t, y[:], c0, c1)
+        def scatter(engine, t, g, c0, c1):
+            target = windows[t][:].indirect(offsets[:, c0 // LIST_ROWS : c1 // LIST_ROWS])
+            if engine is nc.vector:
+                nc.vector.tensor_copy(target, g[:])
+            else:
+                nc.scalar.activation(target, g[:], COPY)
 
-        def vector_scatter(t, g, c0, c1):
-            nc.vector.tensor_copy(windows[t][:].indirect(places(c0, c1)), g[:])
+        out_rows = out_0.rearrange("(l t) u -> l t u", t=PACK)
+        staged = pool.tile([P, PACK, U], F32, name="staged")
 
-        def scalar_scatter(t, g, c0, c1):
-            nc.scalar.activation(windows[t][:].indirect(places(c0, c1)), g[:], COPY)
+        project(0, 0, LEAD, 0)
+        g0_lead = times_gate(nc.vector, 0, 0, LEAD)
+        project(1, 0, LEAD, 1)
+        g1_lead = times_gate(nc.vector, 1, 0, LEAD)
+        project(0, LEAD, T, 2)
+        g0_rest = times_gate(nc.gpsimd, 0, LEAD, T)
+        project(2, 0, T, 3)
+        g2_lead = times_gate(nc.gpsimd, 2, 0, SHARE)
+        project(1, LEAD, T, 4)
+        g1_rest = times_gate(nc.gpsimd, 1, LEAD, T)
+        project(3, 0, T, 5)
+        g3_lead = times_gate(nc.gpsimd, 3, 0, LEAD)
+        g2_rest = times_gate(nc.gpsimd, 2, SHARE, T)
+        g3_rest = times_gate(nc.gpsimd, 3, LEAD, T)
 
-        g0_lead = gated(nc.vector, 0, 0, LEAD, 0)
-        y1 = pool.tile([P, T], F32, name="y1")
-        project(1, 0, SHARE_PROJECTED, 1, y1[:, :SHARE_PROJECTED])
-        g1_lead = times_gate(nc.vector, 1, y1[:, :SHARE], 0, SHARE)
-        g3_lead = gated(nc.gpsimd, 3, 0, LEAD, 3)
-        vector_scatter(0, g0_lead, 0, LEAD)
-        vector_scatter(1, g1_lead, 0, SHARE)
-        vector_scatter(0, gated(nc.gpsimd, 0, LEAD, T, 2), LEAD, T)
-        nc.sync.dma_start(staged[:, 0, :], windows[0][:])
+        scatter(nc.vector, 0, g0_lead, 0, LEAD)
+        scatter(nc.vector, 1, g1_lead, 0, LEAD)
+        scatter(nc.vector, 0, g0_rest, LEAD, T)
+        nc.sync.dma_start(staged[:, 0, :DMA_STAGED], windows[0][:, :DMA_STAGED])
         nc.sync.dma_start(out_rows[:, 0, :], windows[0][:])
-        project(1, SHARE_PROJECTED, T, 4, y1[:, SHARE_PROJECTED:])
-        g1_rest = times_gate(nc.gpsimd, 1, y1[:, SHARE:], SHARE, T)
-        g2 = gated(nc.gpsimd, 2, 0, T, 5)
-        g3_rest = gated(nc.gpsimd, 3, LEAD, T, 6)
-        scalar_scatter(3, g3_lead, 0, LEAD)
-        scalar_scatter(1, g1_rest, SHARE, T)
+        nc.gpsimd.tensor_scalar(staged[:, 0, DMA_STAGED:], windows[0][:, DMA_STAGED:], 1.0, -0.0, MULT, ADD)
+        scatter(nc.scalar, 2, g2_lead, 0, SHARE)
+        scatter(nc.scalar, 1, g1_rest, LEAD, T)
         nc.sync.dma_start(out_rows[:, 1, :], windows[1][:])
         nc.gpsimd.tensor_scalar(staged[:, 1, :], windows[1][:], 1.0, -0.0, MULT, ADD)
-        vector_scatter(2, g2, 0, T)
+        scatter(nc.vector, 3, g3_lead, 0, LEAD)
+        scatter(nc.vector, 2, g2_rest, SHARE, T)
         nc.sync.dma_start(out_rows[:, 2, :], windows[2][:])
-        scalar_scatter(3, g3_rest, LEAD, T)
+        nc.vector.tensor_copy(staged[:, 2, :], windows[2][:])
+        scatter(nc.scalar, 3, g3_rest, LEAD, T)
         nc.sync.dma_start(out_rows[:, 3, :], windows[3][:])
 
         grouped = [pool.tile([P, (b - a) * PACK], BF16, name=f"grouped{a}", align_bytes=64) for a, b in CHUNKS]
         shares = ((nc.vector.tensor_copy, VECTOR_PIECES), (nc.scalar.copy, SCALAR_PIECES))
         for copy, pieces in shares:
-            a, b = pieces[0][0], pieces[-1][1]
-            copy(staged[:, 2, a:b], windows[2][:, a:b])
             for a, b in pieces:
                 copy(staged[:, 3, a:b], windows[3][:, a:b])
         for copy, pieces in shares:
             for a, b in pieces:
-                for tile, (c0, c1) in zip(grouped, CHUNKS):
-                    u0, u1 = max(a, c0), min(b, c1)
-                    if u0 >= u1:
-                        continue
-                    target = tile[:, (u0 - c0) * PACK : (u1 - c0) * PACK]
-                    copy(
-                        target.rearrange("p (g i t) -> p g t i", i=LINE, t=PACK),
-                        staged[:, :, u0:u1].rearrange("p t (g i) -> p g t i", i=LINE),
-                    )
+                tile, c0 = [(tile, c0) for tile, (c0, c1) in zip(grouped, CHUNKS) if c0 <= a < c1][0]
+                copy(
+                    tile[:, (a - c0) * PACK : (b - c0) * PACK].rearrange("p (g i t) -> p g t i", i=LINE, t=PACK),
+                    staged[:, :, a:b].rearrange("p t (g i) -> p g t i", i=LINE),
+                )
 
         o_plane = pool.tile([P, U], U8, name="o_plane", align_bytes=64)
         words_out = out_1[0].rearrange("p u r -> p (u r)").bitcast(I32)

@@ -27,6 +27,7 @@ WIDTHS = (128, 256, 512)
 LEAD = 128
 SHARE = 128
 DMA_STAGED = 512
+SHADOW = 800
 CHUNKS = ((0, 256), (256, 640), (640, 896), (896, 1024))
 VECTOR_PIECES = ((0, 256), (256, 544))
 SCALAR_PIECES = ((544, 640), (640, 896), (896, 1024))
@@ -55,9 +56,15 @@ def tile_picked_wroute2_lingelu_lo_kernel(
         w_rows = w1.rearrange("(p j) n -> p j n", j=PACK)
         for h in range(2):
             nc.sync.dma_start(w_raw[h][:], w_rows[:, :, h * N // 2 : (h + 1) * N // 2])
-        nc.sync.dma_start(x_codes[:].bitcast(I32), x_words[0].rearrange("p n r -> p (n r)").bitcast(I32))
-        nc.sync.dma_start(offsets[:], dst)
+        x_rows = x_words[0].rearrange("p n r -> p (n r)").bitcast(I32)
+        nc.sync.dma_start(x_codes[:, :LEAD].bitcast(I32), x_rows[:, :LEAD])
+        nc.sync.dma_start(x_codes[:, LEAD:].bitcast(I32), x_rows[:, LEAD:])
         nc.sync.dma_start(gate_sb[:], gate)
+        nc.sync.dma_start(offsets[:], dst)
+
+        warm = pool.tile([P, 2], F32, name="warm")
+        nc.vector.memset(warm[:, :1], 0.0)
+        nc.scalar.activation(warm[:, 1:], warm[:, :1], GELU)
 
         for t in range(PACK - 1):
             (nc.vector if t < 2 else nc.gpsimd).memset(windows[t][:], 0.0)
@@ -65,9 +72,9 @@ def tile_picked_wroute2_lingelu_lo_kernel(
         w_codes = [pool.tile([P, P], U32, name=f"w_codes{t}", align_bytes=64) for t in range(PACK)]
         w_planes = [pool.tile([P, P], U8, name=f"w_plane{t}", align_bytes=64) for t in range(PACK)]
 
-        def quantize_weights(h, t0, t1):
+        def quantize_weights(copy, h, t0, t1):
             rounded = pool.tile([P, t1 - t0, HALF * PACK], BF16, name=f"w_rounded{h}_{t0}", tag=f"w_rounded{h}_{t0}", align_bytes=64)
-            nc.vector.tensor_copy(
+            copy(
                 rounded[:].rearrange("p t (l j) -> p l j t", j=PACK),
                 w_raw[h][:].rearrange("p j (l t) -> p l j t", t=PACK)[:, :, :, t0:t1],
             )
@@ -77,9 +84,9 @@ def tile_picked_wroute2_lingelu_lo_kernel(
                     out=w_codes[t][:, cols].bitcast(FP8X4), scales=w_planes[t][:, cols], in_=rounded[:, t - t0, :]
                 )
 
-        quantize_weights(0, 0, PACK)
-        for t0, t1 in ((0, 2), (2, PACK)):
-            quantize_weights(1, t0, t1)
+        quantize_weights(nc.vector.tensor_copy, 0, 0, PACK)
+        quantize_weights(nc.vector.tensor_copy, 1, 0, 2)
+        quantize_weights(nc.scalar.copy, 1, 2, PACK)
         windows.append(pool.tile([P, U], F32, name="window3", tag="w_rounded1_2", align_bytes=64))
         nc.gpsimd.memset(windows[3][:], 0.0)
 
@@ -121,15 +128,19 @@ def tile_picked_wroute2_lingelu_lo_kernel(
         g0_lead = times_gate(nc.vector, 0, 0, LEAD)
         project(1, 0, LEAD, 1)
         g1_lead = times_gate(nc.vector, 1, 0, LEAD)
-        project(0, LEAD, T, 2)
+        project(0, LEAD, T // 2, 2)
+        project(0, T // 2, T, 3)
         g0_rest = times_gate(nc.gpsimd, 0, LEAD, T)
-        project(2, 0, T, 3)
+        project(2, 0, T // 2, 4)
         g2_lead = times_gate(nc.gpsimd, 2, 0, SHARE)
-        project(1, LEAD, T, 4)
+        project(1, LEAD, T // 2, 5)
+        project(1, T // 2, T, 6)
         g1_rest = times_gate(nc.gpsimd, 1, LEAD, T)
-        project(3, 0, T, 5)
+        project(3, 0, T // 2, 7)
         g3_lead = times_gate(nc.gpsimd, 3, 0, LEAD)
+        project(2, T // 2, T, 0)
         g2_rest = times_gate(nc.gpsimd, 2, SHARE, T)
+        project(3, T // 2, T, 1)
         g3_rest = times_gate(nc.gpsimd, 3, LEAD, T)
 
         scatter(nc.vector, 0, g0_lead, 0, LEAD)
@@ -145,8 +156,9 @@ def tile_picked_wroute2_lingelu_lo_kernel(
         scatter(nc.vector, 3, g3_lead, 0, LEAD)
         scatter(nc.vector, 2, g2_rest, SHARE, T)
         nc.sync.dma_start(out_rows[:, 2, :], windows[2][:])
-        nc.vector.tensor_copy(staged[:, 2, :], windows[2][:])
+        nc.vector.tensor_copy(staged[:, 2, :SHADOW], windows[2][:, :SHADOW])
         scatter(nc.scalar, 3, g3_rest, LEAD, T)
+        nc.scalar.copy(staged[:, 2, SHADOW:], windows[2][:, SHADOW:])
         nc.sync.dma_start(out_rows[:, 3, :], windows[3][:])
 
         grouped = [pool.tile([P, (b - a) * PACK], BF16, name=f"grouped{a}", align_bytes=64) for a, b in CHUNKS]

@@ -46,7 +46,7 @@ def tile_picked_wroute2_lingelu_lo_kernel(
         x_plane = pool.tile([P, T], U8, name="x_plane", align_bytes=64)
         gate_sb = pool.tile([P, T], F32, name="gate_sb")
         w_raw = [pool.tile([P, PACK, N // 2], F32, name=f"w_raw{h}") for h in range(2)]
-        windows = [pool.tile([P, U], F32, name=f"window{t}") for t in range(PACK - 1)]
+        windows = [pool.tile([P, U], F32, name=f"window{t}") for t in range(PACK)]
 
         for q in range(QUADRANTS):
             nc.scalar.dma_start(
@@ -66,29 +66,36 @@ def tile_picked_wroute2_lingelu_lo_kernel(
         nc.vector.memset(warm[:, :1], 0.0)
         nc.scalar.activation(warm[:, 1:], warm[:, :1], GELU)
 
-        for t in range(PACK - 1):
-            (nc.vector if t < 2 else nc.gpsimd).memset(windows[t][:], 0.0)
+        for window in windows:
+            nc.vector.memset(window[:], 0.0)
 
         w_codes = [pool.tile([P, P], U32, name=f"w_codes{t}", align_bytes=64) for t in range(PACK)]
         w_planes = [pool.tile([P, P], U8, name=f"w_plane{t}", align_bytes=64) for t in range(PACK)]
 
-        def quantize_weights(copy, h, t0, t1):
-            rounded = pool.tile([P, t1 - t0, HALF * PACK], BF16, name=f"w_rounded{h}_{t0}", tag=f"w_rounded{h}_{t0}", align_bytes=64)
+        rounded = [pool.tile([P, 2, P * PACK], BF16, name=f"w_rounded{u}", align_bytes=64) for u in range(2)]
+
+        def round_weights(copy, h, u):
             copy(
-                rounded[:].rearrange("p t (l j) -> p l j t", j=PACK),
-                w_raw[h][:].rearrange("p j (l t) -> p l j t", t=PACK)[:, :, :, t0:t1],
+                rounded[u][:].rearrange("p t (l j) -> p l j t", j=PACK)[:, h * HALF : (h + 1) * HALF],
+                w_raw[h][:].rearrange("p j (l t) -> p l j t", t=PACK)[:, :, :, 2 * u : 2 * u + 2],
             )
-            cols = slice(h * HALF, (h + 1) * HALF)
-            for t in range(t0, t1):
+
+        def quantize_weights(h, u):
+            for t in range(2):
                 nc.vector.quantize_mx(
-                    out=w_codes[t][:, cols].bitcast(FP8X4), scales=w_planes[t][:, cols], in_=rounded[:, t - t0, :]
+                    out=w_codes[2 * u + t][:, h * HALF : (h + 1) * HALF].bitcast(FP8X4),
+                    scales=w_planes[2 * u + t][:, h * HALF : (h + 1) * HALF],
+                    in_=rounded[u][:, t, h * HALF * PACK : (h + 1) * HALF * PACK],
                 )
 
-        quantize_weights(nc.vector.tensor_copy, 0, 0, PACK)
-        quantize_weights(nc.vector.tensor_copy, 1, 0, 2)
-        quantize_weights(nc.scalar.copy, 1, 2, PACK)
-        windows.append(pool.tile([P, U], F32, name="window3", tag="w_rounded1_2", align_bytes=64))
-        nc.gpsimd.memset(windows[3][:], 0.0)
+        for u in range(2):
+            round_weights(nc.vector.tensor_copy, 0, u)
+        for u in range(2):
+            quantize_weights(0, u)
+        round_weights(nc.vector.tensor_copy, 1, 0)
+        round_weights(nc.scalar.copy, 1, 1)
+        for u in range(2):
+            quantize_weights(1, u)
 
         y = [pool.tile([P, T], F32, name=f"y{t}") for t in range(PACK)]
 

@@ -135,9 +135,10 @@ def tile_picked_wroute2_lingelu_lo_kernel(
         g0_lead = times_gate(nc.vector, 0, 0, LEAD)
         project(1, 0, LEAD, 1)
         g1_lead = times_gate(nc.vector, 1, 0, LEAD)
-        project(0, LEAD, T // 2, 2)
-        project(0, T // 2, T, 3)
-        g0_rest = times_gate(nc.gpsimd, 0, LEAD, T)
+        g0_rest = pool.tile([P, T - LEAD], F32, name="gated0_rest")
+        for bank, (a, b) in enumerate(((LEAD, T // 2), (T // 2, T)), 2):
+            project(0, a, b, bank)
+            nc.gpsimd.tensor_tensor(g0_rest[:, a - LEAD : b - LEAD], y[0][:, a:b], gate_sb[:, a:b], MULT)
         project(2, 0, T // 2, 4)
         g2_lead = times_gate(nc.gpsimd, 2, 0, SHARE)
         project(1, LEAD, T // 2, 5)

@@ -189,7 +189,7 @@ def tile_picked_wroute2_lingelu_lo_kernel(
             nc.vector.quantize_mx(out=codes[:].bitcast(FP8X4), scales=o_plane[:, c0:c1], in_=tile[:])
             nc.sync.dma_start(words_out[:, c0:c1], codes[:].bitcast(I32))
         for q in range(QUADRANTS):
-            queue = nc.scalar if q < 1 else nc.sync
+            queue = nc.scalar if q < 2 else nc.sync
             queue.dma_start(
                 out_2[0, 4 * q : 4 * q + 4, :].bitcast(I32),
                 o_plane[32 * q : 32 * q + 4, :].bitcast(I32),

@@ -25,7 +25,7 @@ HALF = P // 2
 LINE = 4
 WIDTHS = (128, 256, 512)
 LEAD = 128
-SHARE = 128
+SHARE = 160
 DMA_STAGED = 512
 SHADOW = 800
 CHUNKS = ((0, 256), (256, 640), (640, 896), (896, 1024))
@@ -81,7 +81,7 @@ def tile_picked_wroute2_lingelu_lo_kernel(
             )
 
         def quantize_weights(h, u):
-            for t in range(2):
+            for t in (u, 1 - u):
                 nc.vector.quantize_mx(
                     out=w_codes[2 * u + t][:, h * HALF : (h + 1) * HALF].bitcast(FP8X4),
                     scales=w_planes[2 * u + t][:, h * HALF : (h + 1) * HALF],
@@ -135,24 +135,24 @@ def tile_picked_wroute2_lingelu_lo_kernel(
         g0_lead = times_gate(nc.vector, 0, 0, LEAD)
         project(1, 0, LEAD, 1)
         g1_lead = times_gate(nc.vector, 1, 0, LEAD)
-        g0_rest = pool.tile([P, T - LEAD], F32, name="gated0_rest")
-        for bank, (a, b) in enumerate(((LEAD, T // 2), (T // 2, T)), 2):
-            project(0, a, b, bank)
-            nc.gpsimd.tensor_tensor(g0_rest[:, a - LEAD : b - LEAD], y[0][:, a:b], gate_sb[:, a:b], MULT)
-        project(2, 0, T // 2, 4)
-        g2_lead = times_gate(nc.gpsimd, 2, 0, SHARE)
-        project(1, LEAD, T // 2, 5)
-        project(1, T // 2, T, 6)
-        g1_rest = times_gate(nc.gpsimd, 1, LEAD, T)
-        project(3, 0, T // 2, 7)
+        project(3, 0, LEAD, 2)
         g3_lead = times_gate(nc.gpsimd, 3, 0, LEAD)
+        project(0, LEAD, T // 2, 3)
+        project(0, T // 2, T, 4)
+        g0_rest = times_gate(nc.gpsimd, 0, LEAD, T)
+        project(2, 0, T // 2, 5)
+        g2_lead = times_gate(nc.gpsimd, 2, 0, SHARE)
+        project(1, LEAD, T, 6)
+        g1_rest = times_gate(nc.gpsimd, 1, LEAD, T)
+        project(3, LEAD, T, 7)
+        g3_mid = times_gate(nc.gpsimd, 3, LEAD, T // 2)
         project(2, T // 2, T, 0)
         g2_rest = times_gate(nc.gpsimd, 2, SHARE, T)
-        project(3, T // 2, T, 1)
-        g3_rest = times_gate(nc.gpsimd, 3, LEAD, T)
+        g3_rest = times_gate(nc.gpsimd, 3, T // 2, T)
 
         scatter(nc.vector, 0, g0_lead, 0, LEAD)
-        scatter(nc.vector, 1, g1_lead, 0, LEAD)
+        scatter(nc.vector, 3, g3_lead, 0, LEAD)
+        scatter(nc.scalar, 1, g1_lead, 0, LEAD)
         scatter(nc.vector, 0, g0_rest, LEAD, T)
         nc.sync.dma_start(staged[:, 0, :DMA_STAGED], windows[0][:, :DMA_STAGED])
         nc.sync.dma_start(out_rows[:, 0, :], windows[0][:])
@@ -161,11 +161,11 @@ def tile_picked_wroute2_lingelu_lo_kernel(
         scatter(nc.scalar, 1, g1_rest, LEAD, T)
         nc.sync.dma_start(out_rows[:, 1, :], windows[1][:])
         nc.gpsimd.tensor_scalar(staged[:, 1, :], windows[1][:], 1.0, -0.0, MULT, ADD)
-        scatter(nc.vector, 3, g3_lead, 0, LEAD)
+        scatter(nc.vector, 3, g3_mid, LEAD, T // 2)
         scatter(nc.vector, 2, g2_rest, SHARE, T)
         nc.sync.dma_start(out_rows[:, 2, :], windows[2][:])
         nc.vector.tensor_copy(staged[:, 2, :SHADOW], windows[2][:, :SHADOW])
-        scatter(nc.scalar, 3, g3_rest, LEAD, T)
+        scatter(nc.scalar, 3, g3_rest, T // 2, T)
         nc.scalar.copy(staged[:, 2, SHADOW:], windows[2][:, SHADOW:])
         nc.sync.dma_start(out_rows[:, 3, :], windows[3][:])
 

@@ -80,22 +80,19 @@ def tile_picked_wroute2_lingelu_lo_kernel(
                 w_raw[h][:].rearrange("p j (l t) -> p l j t", t=PACK)[:, :, :, 2 * u : 2 * u + 2],
             )
 
-        def quantize_weights(h, u):
+        def quantize_weights(u, a, b):
             for t in (u, 1 - u):
                 nc.vector.quantize_mx(
-                    out=w_codes[2 * u + t][:, h * HALF : (h + 1) * HALF].bitcast(FP8X4),
-                    scales=w_planes[2 * u + t][:, h * HALF : (h + 1) * HALF],
-                    in_=rounded[u][:, t, h * HALF * PACK : (h + 1) * HALF * PACK],
+                    out=w_codes[2 * u + t][:, a:b].bitcast(FP8X4),
+                    scales=w_planes[2 * u + t][:, a:b],
+                    in_=rounded[u][:, t, a * PACK : b * PACK],
                 )
 
-        for u in range(2):
-            round_weights(nc.vector.tensor_copy, 0, u)
-        for u in range(2):
-            quantize_weights(0, u)
-        round_weights(nc.vector.tensor_copy, 1, 0)
-        round_weights(nc.scalar.copy, 1, 1)
-        for u in range(2):
-            quantize_weights(1, u)
+        for h in range(2):
+            round_weights(nc.vector.tensor_copy, h, 0)
+            round_weights(nc.scalar.copy, h, 1)
+            quantize_weights(0, h * HALF, (h + 1) * HALF)
+        quantize_weights(1, 0, P)
 
         y = [pool.tile([P, T], F32, name=f"y{t}") for t in range(PACK)]
 

@@ -22,6 +22,7 @@ PACK = 4
 QUADRANTS = 4
 LIST_ROWS = 16
 HALF = P // 2
+W_LOADS = ((0, 0, 4), (1, 0, 2), (1, 2, 4))
 LINE = 4
 WIDTHS = (128, 256, 512)
 LEAD = 128
@@ -45,7 +46,7 @@ def tile_picked_wroute2_lingelu_lo_kernel(
         x_codes = pool.tile([P, T], U32, name="x_codes", align_bytes=64)
         x_plane = pool.tile([P, T], U8, name="x_plane", align_bytes=64)
         gate_sb = pool.tile([P, T], F32, name="gate_sb")
-        w_raw = [pool.tile([P, PACK, N // 2], F32, name=f"w_raw{h}") for h in range(2)]
+        w_raw = [pool.tile([P, j1 - j0, N // 2], F32, name=f"w_raw{h}_{j0}") for h, j0, j1 in W_LOADS]
         windows = [pool.tile([P, U], F32, name=f"window{t}") for t in range(PACK)]
 
         for q in range(QUADRANTS):
@@ -54,8 +55,8 @@ def tile_picked_wroute2_lingelu_lo_kernel(
                 x_scales[0, 4 * q : 4 * q + 4, :].bitcast(I32),
             )
         w_rows = w1.rearrange("(p j) n -> p j n", j=PACK)
-        for h in range(2):
-            nc.sync.dma_start(w_raw[h][:], w_rows[:, :, h * N // 2 : (h + 1) * N // 2])
+        for raw, (h, j0, j1) in zip(w_raw, W_LOADS):
+            nc.sync.dma_start(raw[:], w_rows[:, j0:j1, h * N // 2 : (h + 1) * N // 2])
         x_rows = x_words[0].rearrange("p n r -> p (n r)").bitcast(I32)
         nc.sync.dma_start(x_codes[:, :LEAD].bitcast(I32), x_rows[:, :LEAD])
         nc.sync.dma_start(x_codes[:, LEAD:].bitcast(I32), x_rows[:, LEAD:])
@@ -74,10 +75,14 @@ def tile_picked_wroute2_lingelu_lo_kernel(
 
         rounded = [pool.tile([P, 2, P * PACK], BF16, name=f"w_rounded{u}", align_bytes=64) for u in range(2)]
 
-        def round_weights(copy, h, u):
+        def round_weights(copy, load, t0, t1):
+            h, j0, j1 = W_LOADS[load]
+            u = t0 // 2
             copy(
-                rounded[u][:].rearrange("p t (l j) -> p l j t", j=PACK)[:, h * HALF : (h + 1) * HALF],
-                w_raw[h][:].rearrange("p j (l t) -> p l j t", t=PACK)[:, :, :, 2 * u : 2 * u + 2],
+                rounded[u][:].rearrange("p t (l j) -> p l j t", j=PACK)[
+                    :, h * HALF : (h + 1) * HALF, j0:j1, t0 - 2 * u : t1 - 2 * u
+                ],
+                w_raw[load][:].rearrange("p j (l t) -> p l j t", t=PACK)[:, :, :, t0:t1],
             )
 
         def quantize_weights(u, a, b):
@@ -88,10 +93,14 @@ def tile_picked_wroute2_lingelu_lo_kernel(
                     in_=rounded[u][:, t, a * PACK : b * PACK],
                 )
 
-        for h in range(2):
-            round_weights(nc.vector.tensor_copy, h, 0)
-            round_weights(nc.scalar.copy, h, 1)
-            quantize_weights(0, h * HALF, (h + 1) * HALF)
+        for load in range(len(W_LOADS)):
+            round_weights(nc.scalar.copy, load, 2, 4)
+        round_weights(nc.vector.tensor_copy, 0, 0, 2)
+        quantize_weights(0, 0, HALF)
+        round_weights(nc.vector.tensor_copy, 1, 0, 2)
+        round_weights(nc.vector.tensor_copy, 2, 0, 1)
+        round_weights(nc.vector.tensor_copy, 2, 1, 2)
+        quantize_weights(0, HALF, P)
         quantize_weights(1, 0, P)
 
         y = [pool.tile([P, T], F32, name=f"y{t}") for t in range(PACK)]

from contextlib import ExitStack

import concourse.mybir as mybir

K, T, N, U = 512, 512, 512, 1024
FLOPS = 2 * K * T * N

F32 = mybir.dt.float32
BF16 = mybir.dt.bfloat16
I32 = mybir.dt.int32
U32 = mybir.dt.uint32
U16 = mybir.dt.uint16
U8 = mybir.dt.uint8
FP8X4 = mybir.dt.float8_e4m3fn_x4
GELU = mybir.ActivationFunctionType.Gelu_apprx_tanh
COPY = mybir.ActivationFunctionType.Copy
MULT = mybir.AluOpType.mult
ADD = mybir.AluOpType.add

P = 128
PACK = 4
QUADRANTS = 4
LIST_ROWS = 16
HALF = P // 2
W_LOADS = ((0, 0, 4), (1, 0, 2), (1, 2, 4))
LINE = 4
WIDTHS = (128, 256, 512)
LEAD = 128
SHARE = 160
DMA_STAGED = 512
SHADOW = 800
CHUNKS = ((0, 256), (256, 640), (640, 896), (896, 1024))
VECTOR_PIECES = ((0, 256), (256, 544))
SCALAR_PIECES = ((544, 640), (640, 896), (896, 1024))


def tile_picked_wroute2_lingelu_lo_kernel(
    tc, x_words, x_scales, gate, w1, dst, out_0, out_1, out_2
):
    nc = tc.nc
    with ExitStack() as ctx:
        pool = ctx.enter_context(tc.tile_pool(name="pool", bufs=1))
        psum = ctx.enter_context(tc.psum_pool(name="psum", bufs=1))

        offsets = pool.tile([P, T // LIST_ROWS], U16, name="offsets")
        x_codes = pool.tile([P, T], U32, name="x_codes", align_bytes=64)
        x_plane = pool.tile([P, T], U8, name="x_plane", align_bytes=64)
        gate_sb = pool.tile([P, T], F32, name="gate_sb")
        w_raw = [pool.tile([P, j1 - j0, N // 2], F32, name=f"w_raw{h}_{j0}") for h, j0, j1 in W_LOADS]
        windows = [pool.tile([P, U], F32, name=f"window{t}") for t in range(PACK)]

        for q in range(QUADRANTS):
            nc.scalar.dma_start(
                x_plane[32 * q : 32 * q + 4, :].bitcast(I32),
                x_scales[0, 4 * q : 4 * q + 4, :].bitcast(I32),
            )
        w_rows = w1.rearrange("(p j) n -> p j n", j=PACK)
        for raw, (h, j0, j1) in zip(w_raw, W_LOADS):
            nc.sync.dma_start(raw[:], w_rows[:, j0:j1, h * N // 2 : (h + 1) * N // 2])
        x_rows = x_words[0].rearrange("p n r -> p (n r)").bitcast(I32)
        nc.sync.dma_start(x_codes[:, :LEAD].bitcast(I32), x_rows[:, :LEAD])
        nc.sync.dma_start(x_codes[:, LEAD:].bitcast(I32), x_rows[:, LEAD:])
        nc.sync.dma_start(gate_sb[:], gate)
        nc.sync.dma_start(offsets[:], dst)

        warm = pool.tile([P, 2], F32, name="warm")
        nc.vector.memset(warm[:, :1], 0.0)
        nc.scalar.activation(warm[:, 1:], warm[:, :1], GELU)

        for window in windows:
            nc.vector.memset(window[:], 0.0)

        w_codes = [pool.tile([P, P], U32, name=f"w_codes{t}", align_bytes=64) for t in range(PACK)]
        w_planes = [pool.tile([P, P], U8, name=f"w_plane{t}", align_bytes=64) for t in range(PACK)]

        rounded = [pool.tile([P, 2, P * PACK], BF16, name=f"w_rounded{u}", align_bytes=64) for u in range(2)]

        def round_weights(copy, load, t0, t1):
            h, j0, j1 = W_LOADS[load]
            u = t0 // 2
            copy(
                rounded[u][:].rearrange("p t (l j) -> p l j t", j=PACK)[
                    :, h * HALF : (h + 1) * HALF, j0:j1, t0 - 2 * u : t1 - 2 * u
                ],
                w_raw[load][:].rearrange("p j (l t) -> p l j t", t=PACK)[:, :, :, t0:t1],
            )

        def quantize_weights(u, a, b):
            for t in (u, 1 - u):
                nc.vector.quantize_mx(
                    out=w_codes[2 * u + t][:, a:b].bitcast(FP8X4),
                    scales=w_planes[2 * u + t][:, a:b],
                    in_=rounded[u][:, t, a * PACK : b * PACK],
                )

        for load in range(len(W_LOADS)):
            round_weights(nc.scalar.copy, load, 2, 4)
        round_weights(nc.vector.tensor_copy, 0, 0, 2)
        quantize_weights(0, 0, HALF)
        round_weights(nc.vector.tensor_copy, 1, 0, 2)
        round_weights(nc.vector.tensor_copy, 2, 0, 1)
        round_weights(nc.vector.tensor_copy, 2, 1, 2)
        quantize_weights(0, HALF, P)
        quantize_weights(1, 0, P)

        y = [pool.tile([P, T], F32, name=f"y{t}") for t in range(PACK)]

        def project(t, c0, c1, bank):
            acc = psum.tile([P, c1 - c0], F32, name=f"acc{t}_{c0}", tag=f"bank{bank}")
            a = c0
            while a < c1:
                step = max(n for n in WIDTHS if n <= c1 - a)
                nc.tensor.matmul_mx(
                    out=acc[:, a - c0 : a - c0 + step],
                    lhsT=w_codes[t][:].bitcast(FP8X4),
                    lhsT_scale=w_planes[t][:],
                    rhs=x_codes[:, a : a + step].bitcast(FP8X4),
                    rhs_scale=x_plane[:, a : a + step],
                    start=True,
                    stop=True,
                )
                a = a + step
            nc.scalar.activation(y[t][:, c0:c1], acc[:], GELU)

        def times_gate(engine, t, c0, c1):
            g = pool.tile([P, c1 - c0], F32, name=f"gated{t}_{c0}")
            engine.tensor_tensor(g[:], y[t][:, c0:c1], gate_sb[:, c0:c1], MULT)
            return g

        def scatter(engine, t, g, c0, c1):
            target = windows[t][:].indirect(offsets[:, c0 // LIST_ROWS : c1 // LIST_ROWS])
            if engine is nc.vector:
                nc.vector.tensor_copy(target, g[:])
            else:
                nc.scalar.activation(target, g[:], COPY)

        out_rows = out_0.rearrange("(l t) u -> l t u", t=PACK)
        staged = pool.tile([P, PACK, U], F32, name="staged")

        project(0, 0, LEAD, 0)
        g0_lead = times_gate(nc.vector, 0, 0, LEAD)
        project(1, 0, LEAD, 1)
        g1_lead = times_gate(nc.vector, 1, 0, LEAD)
        project(3, 0, LEAD, 2)
        g3_lead = times_gate(nc.gpsimd, 3, 0, LEAD)
        project(0, LEAD, T // 2, 3)
        project(0, T // 2, T, 4)
        g0_rest = times_gate(nc.gpsimd, 0, LEAD, T)
        project(2, 0, T // 2, 5)
        g2_lead = times_gate(nc.gpsimd, 2, 0, SHARE)
        project(1, LEAD, T, 6)
        g1_rest = times_gate(nc.gpsimd, 1, LEAD, T)
        project(3, LEAD, T, 7)
        g3_mid = times_gate(nc.gpsimd, 3, LEAD, T // 2)
        project(2, T // 2, T, 0)
        g2_rest = times_gate(nc.gpsimd, 2, SHARE, T)
        g3_rest = times_gate(nc.gpsimd, 3, T // 2, T)

        scatter(nc.vector, 0, g0_lead, 0, LEAD)
        scatter(nc.vector, 3, g3_lead, 0, LEAD)
        scatter(nc.scalar, 1, g1_lead, 0, LEAD)
        scatter(nc.vector, 0, g0_rest, LEAD, T)
        nc.sync.dma_start(staged[:, 0, :DMA_STAGED], windows[0][:, :DMA_STAGED])
        nc.sync.dma_start(out_rows[:, 0, :], windows[0][:])
        nc.gpsimd.tensor_scalar(staged[:, 0, DMA_STAGED:], windows[0][:, DMA_STAGED:], 1.0, -0.0, MULT, ADD)
        scatter(nc.scalar, 2, g2_lead, 0, SHARE)
        scatter(nc.scalar, 1, g1_rest, LEAD, T)
        nc.sync.dma_start(out_rows[:, 1, :], windows[1][:])
        nc.gpsimd.tensor_scalar(staged[:, 1, :], windows[1][:], 1.0, -0.0, MULT, ADD)
        scatter(nc.vector, 3, g3_mid, LEAD, T // 2)
        scatter(nc.vector, 2, g2_rest, SHARE, T)
        nc.sync.dma_start(out_rows[:, 2, :], windows[2][:])
        nc.vector.tensor_copy(staged[:, 2, :SHADOW], windows[2][:, :SHADOW])
        scatter(nc.scalar, 3, g3_rest, T // 2, T)
        nc.scalar.copy(staged[:, 2, SHADOW:], windows[2][:, SHADOW:])
        nc.sync.dma_start(out_rows[:, 3, :], windows[3][:])

        grouped = [pool.tile([P, (b - a) * PACK], BF16, name=f"grouped{a}", align_bytes=64) for a, b in CHUNKS]
        shares = ((nc.vector.tensor_copy, VECTOR_PIECES), (nc.scalar.copy, SCALAR_PIECES))
        for copy, pieces in shares:
            for a, b in pieces:
                copy(staged[:, 3, a:b], windows[3][:, a:b])
        for copy, pieces in shares:
            for a, b in pieces:
                tile, c0 = [(tile, c0) for tile, (c0, c1) in zip(grouped, CHUNKS) if c0 <= a < c1][0]
                copy(
                    tile[:, (a - c0) * PACK : (b - c0) * PACK].rearrange("p (g i t) -> p g t i", i=LINE, t=PACK),
                    staged[:, :, a:b].rearrange("p t (g i) -> p g t i", i=LINE),
                )

        o_plane = pool.tile([P, U], U8, name="o_plane", align_bytes=64)
        words_out = out_1[0].rearrange("p u r -> p (u r)").bitcast(I32)
        for tile, (c0, c1) in zip(grouped, CHUNKS):
            codes = pool.tile([P, c1 - c0], U32, name=f"o_codes{c0}", align_bytes=64)
            nc.vector.quantize_mx(out=codes[:].bitcast(FP8X4), scales=o_plane[:, c0:c1], in_=tile[:])
            nc.sync.dma_start(words_out[:, c0:c1], codes[:].bitcast(I32))
        for q in range(QUADRANTS):
            queue = nc.scalar if q < 2 else nc.sync
            queue.dma_start(
                out_2[0, 4 * q : 4 * q + 4, :].bitcast(I32),
                o_plane[32 * q : 32 * q + 4, :].bitcast(I32),
            )
